import numpy as np, ml_dtypes
CORES = [66,74,82,90,194,202,210,218]
N = 8
import mx_ref
BF = ml_dtypes.bfloat16
def gcols(t, e):
    v = np.concatenate([t.reshape(8, 16, -1, 4), np.zeros((8, 16, 1, 4), BF)], axis=2)
    return np.ascontiguousarray(np.stack([v[g][:, e[g]] for g in range(8)])).reshape(128, -1)
def tile(rs):
    return np.stack(rs, axis=2).reshape(128, -1).astype(BF)
def cut(t, i, w=512):
    return t[:, w * i:w * i + w]
def pick(q, e):
    c = np.concatenate([q[0].reshape(128, -1, 4), np.zeros((128, 1, 4), np.uint8)], axis=1); s = np.concatenate([q[1], np.ones((16, 1), np.uint8)], axis=1)
    return (np.ascontiguousarray(c[:, e].reshape(128, -1)), np.ascontiguousarray(s[:, e]))
def join(*qs):
    return (np.concatenate([q[0] for q in qs], axis=1), np.concatenate([q[1] for q in qs], axis=1))
def put(q, e, v):
    c, s = q[0].reshape(128, -1, 4).copy(), q[1].copy(); c[:, e] = v[0].reshape(128, -1, 4); s[:, e] = v[1]
    return (c.reshape(128, -1), s)
def pk(c, s):
    return (np.ascontiguousarray(c), mx_ref.live(s))
def emit(q):
    return q[0], q[1]
def packed(v, rng):
    q = [mx_ref.quantize(np.ascontiguousarray(v[r])) for r in range(N)]
    return np.stack([a for a, b in q]), np.stack([mx_ref.plane(b, rng) for a, b in q])
def f(rng, *shape):
    return mx_ref.flush((rng.standard_normal(shape, dtype=np.float32) * np.exp2(rng.integers(-2, 3, shape[:-1] + (1,)))).astype(BF))
def wide(rng, *shape, cols=0):
    v = rng.standard_normal(shape, dtype=np.float32) * np.exp2(rng.integers(-12, 13, shape)).astype(np.float32)
    if cols: v *= np.repeat(np.exp2(rng.integers(-cols, cols + 1, shape[:-2] + (1, shape[-1] // 4))) * (rng.random(shape[:-2] + (1, shape[-1] // 4)) > 0.0625), 4, axis=-1).astype(np.float32)
    return mx_ref.flush(v.astype(BF))
C, R = 192, 3
H = C // 2
STEP = [1, 2, 4]
def keep(t, gs):
    v = np.zeros((8, 16, t.shape[1]), BF)
    v[gs] = t.reshape(8, 16, -1)[gs]
    return v.reshape(128, -1)
def grams(a, b):
    n = a.shape[1] // 4
    qa = mx_ref.quantize(np.concatenate([keep(a, [m, m + 4]) for m in range(4)], axis=1))
    qb = mx_ref.quantize(np.concatenate([keep(b, [0, 1, 2, 3]), keep(b, [4, 5, 6, 7])], axis=1))
    z = np.zeros((8, n), np.float32)
    j = np.arange(32)
    for k in range(n // 32):
        e = 32 * k + j
        p = mx_ref.matmul(pick(qa, np.concatenate([e + n * m for m in range(4)])), pick(qb, np.concatenate([e, e + n])))
        for g in range(8): z[g, e] = p[32 * (g % 4) + j, 32 * (g // 4) + j]
    return z + np.float32(0.0)
def over(v):
    return np.repeat(np.repeat(v, 16, axis=0), 4, axis=1)
def big(v):
    v = v.astype(np.float32)
    v[np.abs(v) < np.float32(2.0 ** -16)] = 0
    return v.astype(BF)
def common(w, rng):
    c, p = packed(np.stack([w] * N), rng)
    return {"wc": c, "ws": p}
def weights(rng):
    return common(big(f(rng, 128, 2048)), rng)
def still(rng):
    w = np.zeros((128, 4, 128, 4), np.float32)
    i = np.arange(128)
    for b in range(4): w[i, b, i, b] = 32
    return common(w.reshape(128, 2048).astype(BF), rng)
def numbers_of(rng):
    return {"x": big(f(rng, N, 128, 4 * C)), "v": np.array(f(rng, N, 128, 512))}
def setup_inputs(rng):
    return {**numbers_of(rng), **weights(rng)}
def setup_inputs_ties(rng):
    d = numbers_of(rng)
    x = d["x"].reshape(N, 128, C, 4)
    o = rng.permutation(N)
    for r in range(N):
        k = np.zeros(C, int) if o[r] == 0 else rng.permutation(C) % 3
        a = x[r][:, :3].astype(np.float32)
        a[:, 2] = 0
        z = rng.choice([-1.0, 1.0], (128, 6, 4)).astype(np.float32)
        z[:, 5] = -z[:, 0]
        x[r] = (a[:, k] * z[:, rng.integers(0, 6, C)]).astype(BF)
        if o[r] == 1: x[r] = 0
    return {"x": x.reshape(N, 128, 4 * C), "v": d["v"], **weights(rng)}
def setup_inputs_near(rng):
    main = np.array([[0.75, 0.5, 0.25, 0.25, 0.25, 0, 0, 0], [0.25, 0.5, 0.5, 0.5, 0.25, 0.25, 0.25, 0], [0, 1, 0, 0, 0, 0, 0, 0]])
    size = np.where(rng.permutation(N) < N // 2, 2.0 ** -16, 1.0)
    x = np.zeros((N, 8, 16, C, 4))
    i = np.arange(H)
    s = 3 * i // 2
    tiny = 2.0 ** -11
    def fine(s):
        k = (s[:, None] >> np.array([0, 2, 4, 6])) & 3
        return (np.arange(4) < k[:, :, None]) * np.exp2(np.arange(4) - 11.0)[:, None]
    for r in range(N):
        for g in range(8):
            e = rng.permutation(C).reshape(H, 2)
            kind = np.where(i % 2 == 0, rng.integers(0, 2, H), rng.integers(0, 3, H))
            kind[:2] = (r + g) % 2, 2
            top, low = rng.choice([-1.0, 1.0], (2, H))
            z = np.zeros((C, 16, 4))
            z[e[:, 0], 0, 0] = 1
            z[e[:, 0], 8:12] = fine(s)
            z[e[:, 1], :8, 0] = top[:, None] * main[kind]
            z[e[:, 1], 8:12] = (top * low)[:, None, None] * fine(s + (kind == 2))
            for j in (H - 2, H - 1):
                z[e[j]] = 0
                z[e[j, 0], 0, 0] = 2
                z[e[j, 1], :8, 0] = 2 * main[0]
                z[e[j, 0], 8, :2] = tiny
                if j == H - 2:
                    z[e[j, 1], 8, 1:3] = tiny
                else:
                    z[e[j, 1], 8, 2:] = tiny
                    z[e[j], 9, 0] = 2 * tiny
                z[e[j, 1]] *= top[j]
            x[r, g] = z.transpose(1, 0, 2) * size[r]
    return {"x": x.astype(np.float32).reshape(N, 128, 4 * C).astype(BF), "v": np.array(f(rng, N, 128, 512)), **still(rng)}
def setup_inputs_huge(rng):
    o = rng.permutation(N)
    low = np.where(o == 0, 0.98, 0.8)[:, None, None, None, None]
    x = 2.0 ** 30 * (low + (1 - low) * rng.random((N, 8, 16, C, 4)))
    x[o == 0, :, ::8, :, 0] = 2.0 ** 30
    c = rng.choice([-1.0, 1.0], (N, 8, 1, C, 1))
    c[o % 2 == 1] = 1
    c[o % 2 == 0, :, :, ::3] = -1
    return {"x": (x * c).astype(np.float32).reshape(N, 128, 4 * C).astype(BF), "v": np.array(f(rng, N, 128, 512)), **still(rng)}
def setup_inputs_lean(rng):
    h = np.array([0.25, 0.5, 1.0, 2.0])[rng.integers(0, 4, (N, 1, C, 1))]
    o = rng.permutation(N)
    h[o == 0] = 0.125
    h[o == 1] = 4
    c = rng.choice([-1.0, 1.0], (N, 1, C, 1))
    a = rng.choice([-1.0, 1.0], (N, 128, 1, 4)) * (0.5 + rng.random((N, 128, 1, 4)))
    x = c * (a + h * rng.standard_normal((N, 128, C, 4)))
    return {"x": big(x.reshape(N, 128, 4 * C)), "v": np.array(f(rng, N, 128, 512)), **weights(rng)}
def setup_inputs_spread(rng):
    d = setup_inputs(rng)
    d["x"] = big(wide(rng, N, 128, 4 * C, cols=6))
    return d
def check_inputs(d):
    b = []
    for k in ("x", "v"):
        a = np.abs(d[k].astype(np.float32))
        if not (np.isfinite(a).all() and ((a == 0) | (a >= 2.0 ** -30) & (a <= 2.0 ** 30)).all()): b.append("a value of " + k)
    if ((d["wc"] & 127) == 127).any(): b.append("a code of wc")
    if (d["wc"] != d["wc"][:1]).any(): b.append("wc differs between ranks")
    s = [mx_ref.live(p) for p in d["ws"]]
    if any((p != s[0]).any() for p in s): b.append("ws differs between ranks")
    return b
def reference(x, v, wc, ws):
    w = pk(wc[0], ws[0])
    now = np.concatenate([x[r] for r in range(N)], axis=1)
    for t in range(R):
        d = grams(now, now)
        o = np.argsort(d.reshape(8, N, C), axis=2, kind="stable")
        at = o + C * np.arange(N)[:, None]
        even, odd = at[:, :, ::2].reshape(8, -1), at[:, :, 1::2].reshape(8, -1)
        a, b = gcols(now, even), gcols(now, odd)
        da = np.take_along_axis(d, even, axis=1)
        n = grams(a, b)
        c = np.where(np.abs(n) >= np.float32(0.75) * da, np.float32(1.0), np.where(np.abs(n) >= np.float32(0.25) * da, np.float32(0.5), np.float32(0.0))) * np.sign(n)
        left = (b.astype(np.float32) - over(c) * a.astype(np.float32)).astype(BF)
        swap = over(grams(left, left) < da)
        stay, go = np.where(swap, left, a), np.where(swap, a, left)
        q = mx_ref.quantize(np.ascontiguousarray(go))
        came = tile([mx_ref.matmul(pick(w, np.arange(128 * k, 128 * k + 128)), q) * np.float32(0.03125) for k in range(4)])
        now = np.concatenate([z for r in range(N) for z in (cut(stay, r, 4 * H), cut(came, (r - STEP[t]) % N, 4 * H))], axis=1)
    y, ol = np.zeros((N, 128, C), np.float32), np.zeros((N, 8, C), np.float32)
    oc, osc = np.zeros((N, 128, 4 * C), np.uint8), np.zeros((N, 16, C), np.uint8)
    for r in range(N):
        q = mx_ref.quantize(np.ascontiguousarray(cut(now, r, 4 * C)))
        y[r] = mx_ref.matmul(mx_ref.quantize(v[r]), q)
        ol[r] = o[:, r]
        oc[r], osc[r] = emit(q)
    return {"y": y, "ol": ol, "oc": oc, "osc": osc}

@@ -1,0 +1,576 @@
+from concourse.mybir import dt, AluOpType, ActivationFunctionType
+
+C, H, R = 192, 96, 3
+STEP = [1, 2, 4]
+TINY = 2.0 ** -100
+BELOW = 1.0 - 2.0 ** -24
+RADIX = 2.0 ** 20
+HUGE = 2.0 ** 90
+CH = 6
+WK = 2 * H + CH
+WS = H + CH
+ACT_ITEMS0 = 6
+ACT_K = 1
+ACT_S = 3
+ACT_MASKS = 4
+
+F, B, I, U = "float32", "bfloat16", "int32", "uint16"
+X4, U8 = "float8_e4m3fn_x4", "uint8"
+
+
+def _sb(n, d):
+    return ("sbuf", [128, n], d)
+
+
+SCRATCH = {
+    "X": _sb(896, B), "At": _sb(512, B), "Rt": _sb(512, B), "Mt": _sb(512, B), "vt": _sb(512, B), "zt": _sb(512, B),
+    "Gm": _sb(768, B), "Gm2": _sb(768, B), "a0": _sb(768, B), "bc": _sb(768, B), "ro": _sb(768, B), "w2": _sb(768, B),
+    "qg": _sb(192, X4), "sg": _sb(192, U8), "qg2": _sb(192, X4), "sg2": _sb(192, U8),
+    "qw": _sb(512, X4), "sw": _sb(512, U8), "qv": _sb(128, X4), "sv": _sb(128, U8),
+    "ql": _sb(416, X4), "sl": _sb(416, U8),
+    "qxs": _sb(128, X4), "sxs": _sb(128, U8), "qxk": _sb(128, X4), "sxk": _sb(128, U8),
+    "yt": _sb(192, F),
+    "D": _sb(192, F), "E": _sb(192, F), "pre": _sb(96, F), "row": _sb(192, F), "own": _sb(96, F), "ows": _sb(96, F),
+    "ck": _sb(204, F), "cs": _sb(204, F), "cb": _sb(8 * WK, B), "cn": _sb(4 * WK, B), "sn": _sb(6 * WK, B), "jk": _sb(6 * WK, B),
+    "cnt": _sb(16, F), "ork": _sb(12, U), "O": _sb(192, F), "la": _sb(96, F), "lb": _sb(96, F), "ld": _sb(96, F),
+    "oa": _sb(24, U), "ob": _sb(24, U), "od": _sb(6, U), "da": _sb(96, F), "dap": _sb(96, F), "dam": _sb(96, F),
+    "th": _sb(32, F), "cp": _sb(32, B), "cq": _sb(32, F), "ncp": _sb(96, B),
+    "swp": _sb(96, B), "swr": _sb(96, B), "lm": _sb(96, F), "ls": _sb(24, F), "om": _sb(24, U), "oz": _sb(24, U),
+    "ip": _sb(2, I), "ic": _sb(6, I), "irep": _sb(12, I), "colb": _sb(2, B), "r4": _sb(32, B),
+}
+for _k in ("pk0", "pk1", "pk2", "pk3", "pg0", "pg1", "pg2", "py"):
+    SCRATCH[_k] = ("psum", [128, 512], F)
+SCRATCH["qf0"], SCRATCH["sf0"] = _sb(224, X4), _sb(224, U8)
+for _k in range(2, 10):
+    SCRATCH["qf%d" % _k], SCRATCH["sf%d" % _k] = _sb(128, X4), _sb(128, U8)
+for _k in range(10):
+    SCRATCH["qs%d" % _k], SCRATCH["ss%d" % _k] = _sb(384, X4), _sb(384, U8)
+for _k in range(R):
+    SCRATCH["qm%d" % _k], SCRATCH["sm%d" % _k] = _sb(128, X4), _sb(128, U8)
+
+PART = {}
+for _buf, _dt, _names in (
+        ("cf", F, (("col", 16), ("k32", 64), ("eye", 64), ("one", 192), ("r32", 192), ("qq", 24), ("rl", 24), ("u6", 6),
+                   ("n4", 2), ("k16", 112), ("d16", 112), ("g16", 96), ("r16", 96), ("k4", 100), ("d4", 100), ("g4", 96),
+                   ("k6", 96), ("m6", 96), ("mul", 96), ("ka4", 96), ("base", 96), ("b2", 24), ("vals", 192))),
+        ("cu", U, (("op1", 24), ("op2", 24), ("orep", 12), ("oown", 6), ("on4", 2)))):
+    _at = 0
+    for _n, _w in _names:
+        PART[_n] = (_buf, _at, _w)
+        _at += (_w + 7) // 8 * 8
+    SCRATCH[_buf] = _sb(_at, _dt)
+
+NPOOL = 110
+SEMAPHORES = ["c%d" % k for k in range(NPOOL)] + ["d%d" % k for k in range(24)] + ["arr0", "arr1", "arr2", "sent"]
+
+
+def V(name, lo=0, hi=None, step=1):
+    if name in PART:
+        buf, at, w = PART[name]
+        return (buf, at + lo, at + (w if hi is None else hi), step)
+    return (name, lo, SCRATCH[name][1][1] if hi is None else hi, step)
+
+
+def _bits(v):
+    if SCRATCH[v[0]][0] == "psum":
+        return 1
+    if v[3] == 1:
+        return ((1 << (v[2] - v[1])) - 1) << v[1]
+    m = 0
+    for i in range(v[1], v[2], v[3]):
+        m |= 1 << i
+    return m
+
+
+def emit(g, T, ops):
+    queue = {"v": g.vector, "a": g.scalar, "p": g.tensor, "s": g.sync, "g": g}
+    hist, known, at_issue, waits = {}, {}, [], []
+    for k, (eng, fn, rd, wr, kind) in enumerate(ops):
+        deps = set()
+        acc = [(v, SCRATCH[v[0]][0] == "psum") for v in rd] + [(v, True) for v in wr]
+        for v, w in acc:
+            m = _bits(v)
+            for j, mj, wj in hist.get(v[0], []):
+                if (w or wj) and m & mj:
+                    deps.add(j)
+        for v, w in acc:
+            m = _bits(v)
+            old = hist.get(v[0], [])
+            if w:
+                old = [(j, mj & ~m, wj) for j, mj, wj in old if mj & ~m]
+            hist[v[0]] = old + [(k, m, w)]
+        kn = known.get(eng, 0)
+        mine = []
+        if kind != "arrive":
+            for j in sorted(deps, reverse=True):
+                if j != k and not kn >> j & 1:
+                    mine.append(j)
+                    kn |= at_issue[j] | 1 << j
+            known[eng] = kn
+        at_issue.append(kn if kind != "arrive" else 0)
+        waits.append(mine)
+    waiters = {}
+    for k, w in enumerate(waits):
+        for j in w:
+            waiters.setdefault(j, []).append(k)
+    team = {}
+    for j in sorted(waiters):
+        if ops[j][4] == "c":
+            team.setdefault(tuple(waiters[j]), []).append(j)
+    signal, last, count, ndma, tail, sent = {}, [0] * NPOOL, [0] * NPOOL, 0, [], 0
+    for k, (eng, fn, rd, wr, kind) in enumerate(ops):
+        q = queue.get(eng)
+        if kind == "arrive":
+            signal[k] = fn
+            continue
+        seen = []
+        for j in waits[k]:
+            if not any(signal[j] is z for z in seen):
+                seen.append(signal[j])
+                q.wait_ge(signal[j][0], signal[j][1])
+        ins = fn(q)
+        if kind == "remote":
+            sent += ins
+        elif kind == "dma":
+            sem = T.sem["d%d" % ndma]
+            ndma += 1
+            ins.then_inc(sem, 16)
+            signal[k] = (sem, 16)
+            if k not in waiters:
+                tail.append(signal[k])
+        elif k in waiters:
+            if k not in signal:
+                mates = team[tuple(waiters[k])]
+                s = min((z for z in range(NPOOL) if all(last[z] & ~at_issue[j] == 0 for j in mates)), key=lambda z: last[z])
+                last[s] = sum(1 << j for j in mates)
+                count[s] += len(mates)
+                both = (T.sem["c%d" % s], count[s])
+                for j in mates:
+                    signal[j] = both
+            ins.then_inc(signal[k][0], 1)
+    g.wait_ge(T.sem.sent, sent)
+    for sem, n in tail:
+        g.wait_ge(sem, n)
+
+
+def rank_program(g, core, T, topo):
+    rank = T.rank_of(core)
+    if rank is None:
+        return
+    N = len(T.cores)
+    A, ACT = AluOpType, ActivationFunctionType
+    ops = []
+
+    def ap(v):
+        if v[0] == "@":
+            w = ap(v[1])
+            if SCRATCH[v[1][0]][2] == X4:
+                w = w.bitcast(dt.uint32)
+            return w.indirect(ap(v[2]))
+        return T[v[0]][:, v[1]:v[2]] if v[3] == 1 else T[v[0]][:, v[1]:v[2]:v[3]]
+
+    def parts(*vs):
+        out = []
+        for v in vs:
+            if isinstance(v, tuple):
+                out += [v[1], v[2]] if v[0] == "@" else [v]
+        return out
+
+    def arg(s):
+        return ap(s) if isinstance(s, tuple) else s
+
+    def by(win, off):
+        return ("@", win, off)
+
+    def copy(out, src):
+        if out[0] == "@":
+            ops.append(("v", lambda q: q.tensor_copy(ap(out), ap(src)), parts(src, out[2]), [out[1]], "c"))
+        elif SCRATCH[out[0]][2] == X4:
+            ops.append(("v", lambda q: q.tensor_copy(ap(out).bitcast(dt.uint32), ap(src)), parts(src), [out], "c"))
+        else:
+            ops.append(("v", lambda q: q.tensor_copy(ap(out), ap(src)), parts(src), [out], "c"))
+
+    def ts(out, a, s1, o1, s2=None, o2=None):
+        if o2 is None:
+            ops.append(("v", lambda q: q.tensor_scalar(ap(out), ap(a), arg(s1), None, o1), parts(a, s1), [out], "c"))
+        else:
+            ops.append(("v", lambda q: q.tensor_scalar(ap(out), ap(a), arg(s1), arg(s2), o1, o2), parts(a, s1, s2), [out], "c"))
+
+    def tt(out, a, b, o):
+        ops.append(("v", lambda q: q.tensor_tensor(ap(out), ap(a), ap(b), o), parts(a, b), [out], "c"))
+
+    def scan(out, d0, d1, init, o0, o1):
+        ops.append(("v", lambda q: q.tensor_tensor_scan(ap(out), ap(d0), ap(d1), init, o0, o1), parts(d0, d1), [out], "c"))
+
+    def turn(out, a):
+        ops.append(("v", lambda q: q.transpose(ap(out), ap(a)), [a], [out], "c"))
+
+    def fill(out, c):
+        ops.append(("v", lambda q: q.memset(ap(out), c), [], [out], "c"))
+
+    def quant(q_, s_, a):
+        ops.append(("v", lambda q: q.quantize_mx(ap(q_), ap(s_), ap(a)), [a], [q_, s_], "c"))
+
+    def act(out, a, func=ACT.Copy, scale=None, bias=None, acc=None):
+        kw = {}
+        if scale is not None:
+            kw["scale"] = arg(scale)
+        if bias is not None:
+            kw["bias"] = arg(bias)
+        if acc is not None:
+            kw["accum_out"] = ap(acc)
+        ops.append(("a", lambda q: q.activation(ap(out), ap(a), func, **kw), parts(a, scale, bias), parts(out, acc), "c"))
+
+    def mm(out, wq, wsc, xq, xsc):
+        ops.append(("p", lambda q: q.matmul_mx(ap(out), ap(wq), ap(wsc), ap(xq), ap(xsc), True, True), [wq, wsc, xq, xsc], [out], "c"))
+
+    def iota(out, pattern, base=0, cm=0):
+        if SCRATCH[out[0]][2] == I:
+            ops.append(("g", lambda q: q.iota(ap(out), pattern, base, cm), [], [out], "c"))
+        else:
+            ops.append(("g", lambda q: q.iota(ap(out), pattern, base, cm, allow_small_or_imprecise_dtypes=True), [], [out], "c"))
+
+    def first_zero(out, n, w):
+        one = V("one", 0, n * w)
+        ops.append(("g", lambda q: q.affine_select(ap(out), ap(one), [[0, n], [1, w]], A.is_gt, 0.0, 0, 0), [one], [out], "c"))
+
+    def dma(eng, out, src, rd, wr):
+        ops.append((eng, lambda q: q.dma_start(out, src), rd, wr, "dma"))
+
+    def col(k):
+        return V("col", k, k + 1)
+
+    def ends(name, n, w):
+        return V(name, w - 1, n * w, w)
+
+    cA, cH, cQ, cJ, cA4, cT, cE, c6A, c32, cS4, cS16, cS1, c2A, cTH = range(14)
+
+    dma("s", ap(V("X", 0, 768)), T.x[:, :], [], [V("X", 0, 768)])
+    dma("s", ap(V("qw")).bitcast(dt.uint8), T.wc[:, :], [], [V("qw")])
+    dma("s", ap(V("sw")), T.ws[:, :], [], [V("sw")])
+    dma("s", ap(V("vt")), T.v[:, :], [], [V("vt")])
+
+    iota(V("ip", 0, 1), [[0, 1]], 0, 1)
+    iota(V("qq"), [[0, 3], [1, 4], [0, 2]])
+    iota(V("rl"), [[32, 3], [0, 4], [16, 2]])
+    iota(V("k16"), [[0, 7], [1, 16]])
+    iota(V("irep", 0, 6), [[32, 6]], 31)
+    iota(V("irep", 6, 12), [[4, 6]], 3)
+    iota(V("u6"), [[1, 6]])
+    iota(V("n4"), [[128, 2]], 31)
+    iota(V("k6"), [[1, 16], [0, 6]])
+    iota(V("k4"), [[0, 25], [1, 4]])
+    iota(V("k32"), [[0, 2], [1, 32]])
+    iota(V("one"), [[0, 192]], 1)
+    first_zero(V("r32"), 6, 32)
+    first_zero(V("r16"), 6, 16)
+    iota(V("vals"), [[H, 2], [1, 6], [CH, 16]])
+    iota(V("ka4"), [[0, 6], [1, 4], [0, 4]])
+    iota(V("base"), [[32, 24], [0, 4]])
+    iota(V("th"), [[0, 32]])
+    iota(V("a0", 0, 768, 2), [[0, 384]])
+    iota(V("r4"), [[0, 8], [256, 4]])
+    iota(V("zt"), [[0, 512]])
+
+    def same(out, a, c):
+        act(out, a, ACT.Abs, scale=-1.0, bias=c)
+        act(out, out, ACT.Relu, scale=-1.0, bias=1.0)
+
+    fill(V("X", 768, 896), 0.0)
+    fill(V("At", 384, 512), 0.0)
+    for k, (sh, m) in enumerate([(0, 15), (4, 1), (5, 3), (0, 31), (2, 3), (0, 3)]):
+        ts(V("ic", k, k + 1), V("ip", 0, 1), sh, A.logical_shift_right, m, A.bitwise_and)
+    fill(V("Rt", 384, 512), 0.0)
+    copy(V("col", 0, 6), V("ic"))
+    fill(V("Mt", 384, 512), 0.0)
+    ts(col(cE), col(cH), -1.0, A.mult, 1.0, A.add)
+    ts(V("qq"), V("qq"), col(cQ), A.not_equal, 1000.0, A.mult)
+    copy(V("colb", 1, 2), col(cH))
+    copy(V("colb", 0, 1), col(cE))
+    tt(V("rl"), V("rl"), V("qq"), A.add)
+    act(col(c6A), col(cA), scale=float(CH))
+    act(col(c32), col(cA4), scale=32.0)
+    ts(col(cS1), col(cA4), 3.0, A.is_equal, 1.0 / RADIX, A.max)
+    ts(V("op2"), V("rl"), col(cA), A.add, float(C), A.min)
+    ts(V("op1"), V("rl"), col(cA), A.add, float(H), A.min)
+    ts(col(cS16), col(cA), 15.0, A.is_equal, 1.0 / RADIX, A.max)
+    same(V("d16"), V("k16"), col(cA))
+    act(V("g16"), V("d16", 15, 111), ACT.Identity, scale=RADIX - 1.0, bias=1.0)
+    copy(V("orep"), V("irep"))
+    ts(V("oown"), V("u6"), col(c6A), A.add)
+    ts(V("on4"), V("n4"), col(c32), A.add, float(C - 1), A.min)
+    ts(V("m6"), V("k6"), col(cA), A.is_lt, BELOW - 1.0, A.mult)
+    ts(V("mul"), V("k6"), col(cA), A.not_equal)
+
+    def later_b():
+        same(V("d4"), V("k4"), col(cA4))
+        act(V("g4"), V("d4", 3, 99), ACT.Identity, scale=RADIX - 1.0, bias=1.0)
+        act(col(cS4), col(cS1), scale=4.0)
+        act(col(c2A), col(cA), scale=2.0)
+        act(col(cTH), col(cT), scale=HUGE)
+
+    def later_c():
+        act(V("ka4"), V("ka4"), ACT.Abs, scale=-HUGE, bias=col(cTH))
+        act(V("base"), V("base"), ACT.Identity, bias=col(c2A))
+        act(V("b2"), ends("base", 24, 4), ACT.Identity, scale=2.0, bias=1.0)
+
+    REP, CREP = V("orep", 0, 6), V("orep", 6, 12)
+
+    def masks(src, gm, which, eng):
+        for b, h in which:
+            out = V(gm, 256 * b + 128 * h, 256 * b + 128 * h + 128)
+            if eng == "a":
+                act(out, src(b), scale=col(cE if h == 0 else cH))
+            else:
+                ts(out, src(b), V("colb", h, h + 1), A.mult)
+
+    PAIRS = [(b, h) for b in range(3) for h in range(2)]
+
+    def picks(k, qwin, lst, b, e):
+        copy(V("qs%d" % k, 128 * b, 128 * e), by(qwin, V(lst, 8 * b, 8 * e)))
+
+    def spicks(k, swin, lst, b, e):
+        act(V("ss%d" % k, 128 * b, 128 * e), by(swin, V(lst, 8 * b, 8 * e)))
+
+    def products(k, qg, sg, banks):
+        for b in range(3):
+            lo = min(64 * b, 64)
+            mm(V(banks[b], 0, 128), V("qs%d" % k, 128 * b, 128 * b + 128), V("ss%d" % k, 128 * b, 128 * b + 128),
+               V(qg, lo, lo + 128), V(sg, lo, lo + 128))
+
+    def diagonals(banks):
+        for b in range(3):
+            lo = 64 * b - min(64 * b, 64)
+            tt(V("D", 64 * b, 64 * b + 64), V(banks[b], lo, lo + 64), V("eye"), A.mult)
+
+    def sums():
+        scan(V("E"), V("r32"), V("D"), 0.0, A.mult, A.add)
+
+    PG = ["pg0", "pg1", "pg2"]
+
+    def gram(k, full, src, gap=None):
+        qf, sf = V("qf%d" % k), V("sf%d" % k)
+        masks(src, "Gm", PAIRS[6 - ACT_MASKS:], "a")
+        quant(qf, sf, full)
+        masks(src, "Gm", PAIRS[:6 - ACT_MASKS], "v")
+        picks(k, qf, "op1", 0, 2)
+        quant(V("qg"), V("sg"), V("Gm"))
+        picks(k, qf, "op1", 2, 3)
+        spicks(k, sf, "op1", 0, 2)
+        spicks(k, sf, "op1", 2, 3)
+        products(k, "qg", "sg", PG)
+        if gap:
+            gap()
+        diagonals(PG)
+        sums()
+
+    def spread():
+        ts(V("pre"), by(V("E"), REP), TINY, A.max)
+
+    def own_sizes(lo):
+        tt(V("own"), by(V("row", lo, lo + H), V("oown")), V("d16", 16, 112), A.mult)
+
+    def window(buf, lo, tail, scratch, picked=False):
+        if not picked:
+            own_sizes(lo)
+            tt(V(buf, CH, CH + H), V("row", lo, lo + H), V("mul"), A.mult)
+            scan(V(scratch), V("r16"), V("own"), 0.0, A.mult, A.add)
+        copy(V(buf, 0, CH), ends(scratch, CH, 16))
+        ts(V(buf, tail, tail + CH), ends(scratch, CH, 16), BELOW, A.mult)
+
+    def count_act(items):
+        for w, o, lo, n, c in items:
+            act(V("sn", lo, lo + w[2] - w[1]), w, ACT.Sign, scale=-1.0, bias=o)
+        for w, o, lo, n, c in items:
+            act(V("jk", lo, lo + n), V("sn", lo, lo + n), ACT.Relu, acc=V("cnt", c, c + 1))
+
+    def count_dve(items, width):
+        h = width // 2
+
+        def total(k):
+            scan(V("cn", h * k, h * k + h), V("cb", width * k, width * k + h), V("cb", width * k + h, width * k + width), 0.0, A.add, A.add)
+
+        for k, (w, o) in enumerate(items):
+            ts(V("cb", width * k, width * k + width), w, o, A.is_lt)
+            if k:
+                total(k - 1)
+        total(len(items) - 1)
+
+    def item(buf, m, width):
+        return V(buf, m, m + width), V(buf, m, m + 1)
+
+    def xblock(lo):
+        return lambda b: V("X", lo + 128 * b, lo + 128 * b + 128)
+
+    ng = [2]
+    for t in range(R):
+        if t == 0:
+            masks(xblock(0), "Gm", PAIRS[6 - ACT_MASKS:], "a")
+            quant(V("qf0"), V("sf0"), V("X"))
+            masks(xblock(0), "Gm", PAIRS[:6 - ACT_MASKS], "v")
+            masks(xblock(384), "Gm2", PAIRS[:3], "v")
+            quant(V("qg"), V("sg"), V("Gm"))
+            picks(0, V("qf0"), "op2", 0, 3)
+            spicks(0, V("sf0"), "op2", 0, 3)
+            masks(xblock(384), "Gm2", PAIRS[3:], "a")
+            same(V("eye"), V("k32"), col(cJ))
+            products(0, "qg", "sg", ["pk0", "pk1", "pk2"])
+            picks(1, V("qf0", 96, 224), "op1", 0, 3)
+            quant(V("qg2"), V("sg2"), V("Gm2"))
+            spicks(1, V("sf0", 96, 224), "op1", 0, 3)
+            products(1, "qg2", "sg2", PG)
+            later_b()
+            diagonals(["pk0", "pk1", "pk2"])
+            sums()
+            tt(V("mul"), V("mul"), V("m6"), A.add)
+            spread()
+            diagonals(PG)
+            turn(V("row", 0, H), V("pre"))
+            sums()
+            act(V("ck", WS, WS + H), V("row", 0, H), scale=BELOW)
+            own_sizes(0)
+            spread()
+            scan(V("ows"), V("r16"), V("own"), 0.0, A.mult, A.add)
+            turn(V("row", H, C), V("pre"))
+            tt(V("cs", CH, CH + H), V("row", 0, H), V("mul"), A.mult)
+            act(V("cs", WS, WS + H), V("row", H, C))
+            window("cs", 0, WK, "ows", True)
+            na = ACT_ITEMS0
+            count_act([item("cs", m, WK) + (WK * m, WK, m) for m in range(na)])
+            window("ck", H, WK, "la")
+            tt(V("g4"), V("g4"), V("d4", 4, 100), A.subtract)
+            count_dve([item("cs", m, WK) for m in range(na, CH)] + [item("ck", m, WK) for m in range(CH)], WK)
+            tt(V("g16"), V("g16"), V("d16", 16, 112), A.subtract)
+            later_c()
+        else:
+            gram(ng[0], V("X", 384, 896), xblock(384))
+            ng[0] += 1
+            spread()
+            turn(V("row", H, C), V("pre"))
+            na = CH + ACT_K
+            count_act([(V("row", H, C), V("cs", m, m + 1), (H + 1) * m, H + 1, m) for m in range(CH)])
+            window("ck", H, WK, "la")
+            count_act([item("ck", m, WK) + (CH * (H + 1) + WK * m, WK, CH + m) for m in range(ACT_K)])
+            count_dve([item("ck", m, WK) for m in range(ACT_K, CH)], WK)
+        ts(V("ork", na, 12), ends("cn", 12 - na, WK // 2), -float(CH), A.add)
+        ts(V("ork", 0, na), V("cnt", 0, na), -float(CH), A.add)
+        copy(by(V("O"), V("ork")), V("vals"))
+
+        k = ng[0]
+        ng[0] += 1
+        qf, sf = V("qf%d" % k), V("sf%d" % k)
+        scan(V("lb"), V("g4"), V("O", 1, C, 2), 0.0, A.mult, A.add)
+        scan(V("la"), V("g4"), V("O", 0, C, 2), 0.0, A.mult, A.add)
+        ts(V("ob"), ends("lb", 24, 4), col(cS4), A.mult, col(cT), A.add)
+        ts(V("oa"), ends("la", 24, 4), col(cS4), A.mult, col(cT), A.add)
+        act(V("bc", 1, 768, 2), by(V("X", 0, 768), V("ob")))
+        copy(V("At", 0, 384), by(V("X", 0, 768), V("oa")))
+        if t == R - 1:
+            dma("s", T.ol[:, :], T.O[0:128:16, :], [V("O")], [])
+        bblock = lambda b: V("bc", 256 * b + 1, 256 * b + 256, 2)
+        scan(V("ld"), V("g16"), V("O", 0, C, 2), 0.0, A.mult, A.add)
+        quant(qf, sf, V("At"))
+        ts(V("od"), ends("ld", CH, 16), col(cS16), A.mult)
+        masks(bblock, "Gm", PAIRS[6 - ACT_MASKS:], "a")
+        picks(k, qf, "op1", 0, 2)
+        act(V("da"), by(V("row"), V("od")))
+        spicks(k, sf, "op1", 0, 2)
+        spicks(k, sf, "op1", 2, 3)
+        masks(bblock, "Gm", PAIRS[:6 - ACT_MASKS], "v")
+        quant(V("qg"), V("sg"), V("Gm"))
+        picks(k, qf, "op1", 2, 3)
+        turn(V("dap"), V("da"))
+        d6 = V("dap", 0, H, 16)
+        act(V("th", 0, 24, 4), d6, scale=0.75)
+        act(V("th", 1, 24, 4), d6, scale=0.25)
+        act(V("th", 3, 24, 4), V("th", 0, 24, 4), scale=-BELOW)
+        act(V("th", 2, 24, 4), V("th", 1, 24, 4), scale=-BELOW)
+        products(k, "qg", "sg", PG)
+        diagonals(PG)
+        sums()
+
+        act(V("a0", 1, 768, 2), V("At", 0, 384))
+        tt(V("cp"), by(V("E"), V("on4")), V("th"), A.is_ge)
+        scan(V("cq"), V("r4"), V("cp"), 0.0, A.min, A.add)
+        ts(V("ncp"), by(V("cq"), CREP), -0.5, A.mult, 1.0, A.add)
+        act(V("w2", 0, 768, 2), V("At", 0, 384))
+        for e in range(4):
+            turn(V("bc", 2 * e, 768, 8), V("ncp"))
+        scan(V("ro"), V("a0"), V("bc"), 0.0, A.mult, A.add)
+
+        copy(V("Rt", 0, 384), V("ro", 1, 768, 2))
+
+        def gap():
+            act(V("w2", 1, 768, 2), V("Rt", 0, 384))
+            tt(V("dam"), V("dap"), V("ka4"), A.max)
+
+        gram(ng[0], V("Rt"), lambda b: V("ro", 256 * b + 1, 256 * b + 256, 2), gap)
+        ng[0] += 1
+        tt(V("swp"), by(V("E"), REP), V("dam"), A.is_ge)
+        turn(V("swr"), V("swp"))
+        scan(V("lm"), V("base"), V("swr"), 0.0, A.max, A.add)
+        copy(V("om"), ends("lm", 24, 4))
+        copy(V("Mt", 0, 192), by(V("w2"), V("om", 0, 12)))
+        act(V("Mt", 192, 384), by(V("w2"), V("om", 12, 24)))
+        qm, sm = "qm%d" % t, "sm%d" % t
+        quant(V(qm), V(sm), V("Mt"))
+        dst = T.cores[(rank + STEP[t]) % N]
+        rid, pid = topo.addr(dst, core)
+        mask = topo.mask(core, dst)
+        neng = len(topo.engines(core, dst))
+        lo = 128 + H * t
+        arr = T.sem["arr%d" % t]
+
+        def send(out, src, arr=arr, rid=rid, pid=pid, mask=mask, neng=neng):
+            def go(q):
+                q.remote_dma(out, src, arr, T.sem.sent, pid, rid, mask)
+                return neng
+            return go
+
+        ops.append(("g", send(ap(V("ql", lo, lo + H)).bitcast(dt.uint8), ap(V(qm, 0, H)).bitcast(dt.uint8)), [V(qm, 0, H)], [], "remote"))
+        ops.append(("g", send(ap(V("sl", lo, lo + H)), ap(V(sm, 0, H))), [V(sm, 0, H)], [], "remote"))
+        src = T.cores[(rank - STEP[t]) % N]
+        ops.append(("x", (arr, 2 * len(topo.engines(src, core))), [], [V("ql", lo, lo + H), V("sl", lo, lo + H)], "arrive"))
+
+        tt(V("ls"), V("b2"), ends("lm", 24, 4), A.subtract)
+        if t < R - 1:
+            tt(V("pre"), by(V("E"), REP), V("dap"), A.min)
+        copy(V("oz"), V("ls"))
+        if t == 0:
+            quant(V("ql", 0, 128), V("sl", 0, 128), V("zt"))
+        act(V("X", 0, 384), by(V("w2"), V("oz")))
+        if t < R - 1:
+            ts(V("pre"), V("pre"), TINY, A.max)
+            turn(V("row", 0, H), V("pre"))
+            act(V("ck", WS, WS + H), V("row", 0, H), scale=BELOW)
+            window("cs", 0, WS, "ows")
+            at = CH * (H + 1) + WK * ACT_K
+            count_act([item("cs", m, WS) + (at + WS * m, WS, 12 + m) for m in range(ACT_S)])
+            act(V("sn", H, ACT_S * (H + 1), H + 1), V("cnt", 12, 12 + ACT_S))
+            count_dve([item("cs", m, WS) for m in range(ACT_S, CH)], WS)
+            copy(V("sn", ACT_S * (H + 1) + H, CH * (H + 1), H + 1), ends("cn", CH - ACT_S, WS // 2))
+        else:
+            quant(V("qv"), V("sv"), V("vt"))
+            quant(V("qxs"), V("sxs"), V("X", 0, 512))
+            mm(V("py", 0, 128), V("qv"), V("sv"), V("qxs"), V("sxs"))
+            dma("s", T.oc[:, 0:4 * H], ap(V("qxs", 0, H)).bitcast(dt.uint8), [V("qxs")], [])
+            for e in range(4):
+                dma("s", T.osc[4 * e:4 * e + 4, 0:H], T.sxs[32 * e:32 * e + 4, 0:H], [V("sxs")], [])
+            copy(V("yt", 0, H), V("py", 0, H))
+            dma("s", T.y[:, 0:H], ap(V("yt", 0, H)), [V("yt", 0, H)], [])
+
+        for b in (0, 2, 1, 3):
+            mm(V("pk%d" % b, 0, 128), V("qw", 128 * b, 128 * b + 128), V("sw", 128 * b, 128 * b + 128),
+               V("ql", lo - 32, lo + H), V("sl", lo - 32, lo + H))
+        for b in (0, 1):
+            ts(V("X", 384 + b, 768, 4), V("pk%d" % b, 32, 128), 0.03125, A.mult)
+            act(V("X", 386 + b, 768, 4), V("pk%d" % (b + 2), 32, 128), scale=0.03125)
+
+    quant(V("qxk"), V("sxk"), V("X", 384, 896))
+    mm(V("pg0", 0, 128), V("qv"), V("sv"), V("qxk"), V("sxk"))
+    dma("s", T.oc[:, 4 * H:4 * C], ap(V("qxk", 0, H)).bitcast(dt.uint8), [V("qxk")], [])
+    for e in range(4):
+        dma("s" if e < 2 else "a", T.osc[4 * e:4 * e + 4, H:C], T.sxk[32 * e:32 * e + 4, 0:H], [V("sxk")], [])
+    copy(V("yt", H, C), V("pg0", 0, H))
+    dma("a", T.y[:, H:C], ap(V("yt", H, C)), [V("yt", H, C)], [])
+    emit(g, T, ops)

@@ -12,7 +12,7 @@ WS = H + CH
 ACT_ITEMS0 = 6
 ACT_K = 1
 ACT_S = 3
-ACT_MASKS = 4
+ACT_MASKS = 3
 
 F, B, I, U = "float32", "bfloat16", "int32", "uint16"
 X4, U8 = "float8_e4m3fn_x4", "uint8"
@@ -343,26 +343,36 @@ def rank_program(g, core, T, topo):
             lo = 64 * b - min(64 * b, 64)
             tt(V("D", 64 * b, 64 * b + 64), V(banks[b], lo, lo + 64), V("eye"), A.mult)
 
-    def sums():
-        scan(V("E"), V("r32"), V("D"), 0.0, A.mult, A.add)
+    def sums(lo=0, hi=192):
+        scan(V("E", lo, hi), V("r32", lo, hi), V("D", lo, hi), 0.0, A.mult, A.add)
 
     PG = ["pg0", "pg1", "pg2"]
+
+    def extract():
+        diagonals(PG)
+        sums(0, 128)
+        sums(128, 192)
 
     def gram(k, full, src, gap=None):
         qf, sf = V("qf%d" % k), V("sf%d" % k)
         masks(src, "Gm", PAIRS[6 - ACT_MASKS:], "a")
-        quant(qf, sf, full)
-        masks(src, "Gm", PAIRS[:6 - ACT_MASKS], "v")
-        picks(k, qf, "op1", 0, 2)
-        quant(V("qg"), V("sg"), V("Gm"))
+        if gap:
+            masks(src, "Gm", PAIRS[:6 - ACT_MASKS], "v")
+            quant(qf, sf, full)
+            quant(V("qg"), V("sg"), V("Gm"))
+            picks(k, qf, "op1", 0, 2)
+        else:
+            quant(qf, sf, full)
+            masks(src, "Gm", PAIRS[:6 - ACT_MASKS], "v")
+            picks(k, qf, "op1", 0, 2)
+            quant(V("qg"), V("sg"), V("Gm"))
         picks(k, qf, "op1", 2, 3)
         spicks(k, sf, "op1", 0, 2)
         spicks(k, sf, "op1", 2, 3)
         products(k, "qg", "sg", PG)
         if gap:
             gap()
-        diagonals(PG)
-        sums()
+        extract()
 
     def spread():
         ts(V("pre"), by(V("E"), REP), TINY, A.max)
@@ -392,8 +402,9 @@ def rank_program(g, core, T, topo):
 
         for k, (w, o) in enumerate(items):
             ts(V("cb", width * k, width * k + width), w, o, A.is_lt)
-            if k:
-                total(k - 1)
+            if k > 1:
+                total(k - 2)
+        total(len(items) - 2)
         total(len(items) - 1)
 
     def item(buf, m, width):
@@ -452,8 +463,8 @@ def rank_program(g, core, T, topo):
             window("ck", H, WK, "la")
             count_act([item("ck", m, WK) + (CH * (H + 1) + WK * m, WK, CH + m) for m in range(ACT_K)])
             count_dve([item("ck", m, WK) for m in range(ACT_K, CH)], WK)
-        ts(V("ork", na, 12), ends("cn", 12 - na, WK // 2), -float(CH), A.add)
         ts(V("ork", 0, na), V("cnt", 0, na), -float(CH), A.add)
+        ts(V("ork", na, 12), ends("cn", 12 - na, WK // 2), -float(CH), A.add)
         copy(by(V("O"), V("ork")), V("vals"))
 
         k = ng[0]
@@ -464,19 +475,19 @@ def rank_program(g, core, T, topo):
         ts(V("ob"), ends("lb", 24, 4), col(cS4), A.mult, col(cT), A.add)
         ts(V("oa"), ends("la", 24, 4), col(cS4), A.mult, col(cT), A.add)
         act(V("bc", 1, 768, 2), by(V("X", 0, 768), V("ob")))
+        scan(V("ld"), V("g16"), V("O", 0, C, 2), 0.0, A.mult, A.add)
         copy(V("At", 0, 384), by(V("X", 0, 768), V("oa")))
         if t == R - 1:
             dma("s", T.ol[:, :], T.O[0:128:16, :], [V("O")], [])
         bblock = lambda b: V("bc", 256 * b + 1, 256 * b + 256, 2)
-        scan(V("ld"), V("g16"), V("O", 0, C, 2), 0.0, A.mult, A.add)
-        quant(qf, sf, V("At"))
         ts(V("od"), ends("ld", CH, 16), col(cS16), A.mult)
+        quant(qf, sf, V("At"))
+        masks(bblock, "Gm", PAIRS[:6 - ACT_MASKS], "v")
         masks(bblock, "Gm", PAIRS[6 - ACT_MASKS:], "a")
         picks(k, qf, "op1", 0, 2)
         act(V("da"), by(V("row"), V("od")))
         spicks(k, sf, "op1", 0, 2)
         spicks(k, sf, "op1", 2, 3)
-        masks(bblock, "Gm", PAIRS[:6 - ACT_MASKS], "v")
         quant(V("qg"), V("sg"), V("Gm"))
         picks(k, qf, "op1", 2, 3)
         turn(V("dap"), V("da"))
@@ -486,8 +497,7 @@ def rank_program(g, core, T, topo):
         act(V("th", 3, 24, 4), V("th", 0, 24, 4), scale=-BELOW)
         act(V("th", 2, 24, 4), V("th", 1, 24, 4), scale=-BELOW)
         products(k, "qg", "sg", PG)
-        diagonals(PG)
-        sums()
+        extract()
 
         act(V("a0", 1, 768, 2), V("At", 0, 384))
         tt(V("cp"), by(V("E"), V("on4")), V("th"), A.is_ge)
@@ -496,9 +506,11 @@ def rank_program(g, core, T, topo):
         act(V("w2", 0, 768, 2), V("At", 0, 384))
         for e in range(4):
             turn(V("bc", 2 * e, 768, 8), V("ncp"))
-        scan(V("ro"), V("a0"), V("bc"), 0.0, A.mult, A.add)
+        for lo, hi in ((0, 512), (512, 768)):
+            scan(V("ro", lo, hi), V("a0", lo, hi), V("bc", lo, hi), 0.0, A.mult, A.add)
 
-        copy(V("Rt", 0, 384), V("ro", 1, 768, 2))
+        for lo, hi in ((0, 512), (512, 768)):
+            copy(V("Rt", lo // 2, hi // 2), V("ro", lo + 1, hi, 2))
 
         def gap():
             act(V("w2", 1, 768, 2), V("Rt", 0, 384))
@@ -559,7 +571,7 @@ def rank_program(g, core, T, topo):
             copy(V("yt", 0, H), V("py", 0, H))
             dma("s", T.y[:, 0:H], ap(V("yt", 0, H)), [V("yt", 0, H)], [])
 
-        for b in (0, 2, 1, 3):
+        for b in (2, 0, 3, 1):
             mm(V("pk%d" % b, 0, 128), V("qw", 128 * b, 128 * b + 128), V("sw", 128 * b, 128 * b + 128),
                V("ql", lo - 32, lo + H), V("sl", lo - 32, lo + H))
         for b in (0, 1):

@@ -7,12 +7,11 @@ BELOW = 1.0 - 2.0 ** -24
 RADIX = 2.0 ** 20
 HUGE = 2.0 ** 90
 CH = 6
-WK = 2 * H + CH
-WS = H + CH
-ACT_ITEMS0 = 6
-ACT_K = 1
-ACT_S = 3
-ACT_MASKS = 3
+WS = H - 16
+WK = WS + H
+SLOT = 100
+Z = dict(ss=3, sk=4, kk=2, ss0=2, sk0=4, kk0=2, mk=3, ma=4, mr=4, split=1, pre="a", wake=250.0, send=1500.0, load=1400.0,
+         mk0=6, gx=0.5, gm=0.5, boost=100.0)
 
 F, B, I, U = "float32", "bfloat16", "int32", "uint16"
 X4, U8 = "float8_e4m3fn_x4", "uint8"
@@ -23,26 +22,19 @@ def _sb(n, d):
 
 
 SCRATCH = {
-    "X": _sb(896, B), "At": _sb(512, B), "Rt": _sb(512, B), "Mt": _sb(512, B), "vt": _sb(512, B), "zt": _sb(512, B),
-    "Gm": _sb(768, B), "Gm2": _sb(768, B), "a0": _sb(768, B), "bc": _sb(768, B), "ro": _sb(768, B), "w2": _sb(768, B),
-    "qg": _sb(192, X4), "sg": _sb(192, U8), "qg2": _sb(192, X4), "sg2": _sb(192, U8),
+    "X": _sb(896, B), "SX": _sb(776, B), "AR": _sb(776, B), "Mt": _sb(512, B), "vt": _sb(512, B), "zt": _sb(512, B),
     "qw": _sb(512, X4), "sw": _sb(512, U8), "qv": _sb(128, X4), "sv": _sb(128, U8),
     "ql": _sb(416, X4), "sl": _sb(416, U8),
     "qxs": _sb(128, X4), "sxs": _sb(128, U8), "qxk": _sb(128, X4), "sxk": _sb(128, U8),
-    "yt": _sb(192, F),
-    "D": _sb(192, F), "E": _sb(192, F), "pre": _sb(96, F), "row": _sb(192, F), "own": _sb(96, F), "ows": _sb(96, F),
-    "ck": _sb(204, F), "cs": _sb(204, F), "cb": _sb(8 * WK, B), "cn": _sb(4 * WK, B), "sn": _sb(6 * WK, B), "jk": _sb(6 * WK, B),
-    "cnt": _sb(16, F), "ork": _sb(12, U), "O": _sb(192, F), "la": _sb(96, F), "lb": _sb(96, F), "ld": _sb(96, F),
-    "oa": _sb(24, U), "ob": _sb(24, U), "od": _sb(6, U), "da": _sb(96, F), "dap": _sb(96, F), "dam": _sb(96, F),
-    "th": _sb(32, F), "cp": _sb(32, B), "cq": _sb(32, F), "ncp": _sb(96, B),
-    "swp": _sb(96, B), "swr": _sb(96, B), "lm": _sb(96, F), "ls": _sb(24, F), "om": _sb(24, U), "oz": _sb(24, U),
-    "ip": _sb(2, I), "ic": _sb(6, I), "irep": _sb(12, I), "colb": _sb(2, B), "r4": _sb(32, B),
+    "yt": _sb(192, F), "Of": _sb(192, F), "ip": _sb(2, I), "ic": _sb(8, I), "iu": _sb(24, I), "iw": _sb(24, I), "irep": _sb(24, I),
 }
+for _k in "SKAR":
+    SCRATCH["G" + _k], SCRATCH["qg" + _k], SCRATCH["sg" + _k] = _sb(768, B), _sb(192, X4), _sb(192, U8)
 for _k in ("pk0", "pk1", "pk2", "pk3", "pg0", "pg1", "pg2", "py"):
     SCRATCH[_k] = ("psum", [128, 512], F)
 SCRATCH["qf0"], SCRATCH["sf0"] = _sb(224, X4), _sb(224, U8)
 for _k in range(2, 10):
-    SCRATCH["qf%d" % _k], SCRATCH["sf%d" % _k] = _sb(128, X4), _sb(128, U8)
+    SCRATCH["qf%d" % _k], SCRATCH["sf%d" % _k] = _sb(194, X4), _sb(194, U8)
 for _k in range(10):
     SCRATCH["qs%d" % _k], SCRATCH["ss%d" % _k] = _sb(384, X4), _sb(384, U8)
 for _k in range(R):
@@ -50,18 +42,27 @@ for _k in range(R):
 
 PART = {}
 for _buf, _dt, _names in (
-        ("cf", F, (("col", 16), ("k32", 64), ("eye", 64), ("one", 192), ("r32", 192), ("qq", 24), ("rl", 24), ("u6", 6),
-                   ("n4", 2), ("k16", 112), ("d16", 112), ("g16", 96), ("r16", 96), ("k4", 100), ("d4", 100), ("g4", 96),
-                   ("k6", 96), ("m6", 96), ("mul", 96), ("ka4", 96), ("base", 96), ("b2", 24), ("vals", 192))),
-        ("cu", U, (("op1", 24), ("op2", 24), ("orep", 12), ("oown", 6), ("on4", 2)))):
+        ("cf", F, (("col", 32), ("k32", 64), ("eye", 64), ("k2", 64), ("eye2", 64), ("one", 96), ("big", 192), ("r32", 96), ("t32", 192),
+                   ("rl", 24), ("rq", 24), ("opf", 24), ("n4", 2), ("k16", 96), ("s16", 96), ("d16", 96), ("r16", 96), ("k4", 192),
+                   ("mul", 96), ("ka4", 96), ("b2", 24))),
+        ("cb", B, (("colb", 2), ("r4", 32), ("g16", 96), ("g4", 192), ("base", 96), ("vals", 192), ("r16b", 96))),
+        ("cu", U, (("op1", 24), ("op2", 24), ("op3", 24), ("op4", 24), ("orep", 24), ("on4", 2))),
+        ("wf", F, (("DS", 192), ("DK", 192), ("DA", 192), ("DR", 192), ("ES", 192), ("EK", 192), ("EA", 192), ("ER", 192),
+                   ("preS", 96), ("preK", 96), ("prwS", 96), ("prwK", 96), ("row", C + H + WS), ("ownS", 96), ("ownK", 96),
+                   ("owS", 96), ("owK", 96), ("mixS", 96), ("mixK", 96), ("cs", 2 * WS), ("sn", CH * (H + 1)),
+                   ("snS", CH * (WS + 1)), ("snK", CH * (WK + 1)), ("fin", 12 * SLOT), ("inS", 96), ("inK", 96),
+                   ("da", 96), ("dap", 96), ("dam", 96), ("th", 32), ("cq", 32), ("ls", 24))),
+        ("wb", B, (("fs", CH * WS), ("fx", CH * H), ("fk", CH * WK), ("cn", CH * SLOT), ("O", 192), ("lx", 192), ("ld", 96), ("cp", 32),
+                   ("ncp", 96), ("cz", 192), ("swp", 96), ("swr", 96), ("lm", 96), ("fmS", 96), ("fmK", 96))),
+        ("wu", U, (("ork", 12), ("ox", 48), ("od", 6), ("om", 24), ("oz", 24)))):
     _at = 0
     for _n, _w in _names:
         PART[_n] = (_buf, _at, _w)
-        _at += (_w + 7) // 8 * 8
+        _at += (_w + 15) // 16 * 16
     SCRATCH[_buf] = _sb(_at, _dt)
 
-NPOOL = 110
-SEMAPHORES = ["c%d" % k for k in range(NPOOL)] + ["d%d" % k for k in range(24)] + ["arr0", "arr1", "arr2", "sent"]
+NPOOL = 124
+SEMAPHORES = ["c%d" % k for k in range(NPOOL)] + ["d%d" % k for k in range(20)] + ["arr%d" % k for k in range(R)] + ["sent"]
 
 
 def V(name, lo=0, hi=None, step=1):
@@ -82,10 +83,10 @@ def _bits(v):
     return m
 
 
-def emit(g, T, ops):
-    queue = {"v": g.vector, "a": g.scalar, "p": g.tensor, "s": g.sync, "g": g}
-    hist, known, at_issue, waits = {}, {}, [], []
-    for k, (eng, fn, rd, wr, kind) in enumerate(ops):
+def needs(ops):
+    hist, out = {}, []
+    for k, op in enumerate(ops):
+        rd, wr = op[2], op[3]
         deps = set()
         acc = [(v, SCRATCH[v[0]][0] == "psum") for v in rd] + [(v, True) for v in wr]
         for v, w in acc:
@@ -99,11 +100,58 @@ def emit(g, T, ops):
             if w:
                 old = [(j, mj & ~m, wj) for j, mj, wj in old if mj & ~m]
             hist[v[0]] = old + [(k, m, w)]
+        deps.discard(k)
+        out.append(deps)
+    return out
+
+
+def arrange(ops, deps):
+    n = len(ops)
+    late = {"dma": Z["load"], "remote": 0.0, "arrive": 0.0, "c": 0.0}
+    after = [[] for _ in ops]
+    for k, d in enumerate(deps):
+        for j in d:
+            after[j].append(k)
+    chain = [0.0] * n
+    for k in range(n - 1, -1, -1):
+        chain[k] = ops[k][5] + late[ops[k][4]] + max([Z["wake"] + chain[j] for j in after[k]], default=0.0)
+    left = [len(d) for d in deps]
+    due = [0.0] * n
+    ready = {k for k in range(n) if not left[k]}
+    free, order = {}, []
+    while ready:
+        start = {k: max(due[k], free.get(ops[k][0], 0.0)) for k in ready}
+        first = min(ready, key=lambda k: (start[k] + ops[k][5], k))
+        end = start[first] + ops[first][5]
+        k = max((j for j in ready if ops[j][0] == ops[first][0] and start[j] < end), key=lambda j: (chain[j] + ops[j][6], -j))
+        if ops[k][0] != "x":
+            free[ops[k][0]] = start[k] + ops[k][5]
+        done = start[k] + ops[k][5] + late[ops[k][4]] + Z["wake"]
+        ready.discard(k)
+        order.append(k)
+        for j in after[k]:
+            left[j] -= 1
+            due[j] = max(due[j], done)
+            if not left[j]:
+                ready.add(j)
+    return order
+
+
+def emit(g, T, ops):
+    queue = {"v": g.vector, "a": g.scalar, "p": g.tensor, "s": g.sync, "g": g}
+    deps = needs(ops)
+    order = arrange(ops, deps)
+    place = {k: i for i, k in enumerate(order)}
+    deps = [{place[j] for j in deps[k]} for k in order]
+    ops = [ops[k] for k in order]
+    known, at_issue, waits = {}, [], []
+    for k, op in enumerate(ops):
+        eng, kind = op[0], op[4]
         kn = known.get(eng, 0)
         mine = []
         if kind != "arrive":
-            for j in sorted(deps, reverse=True):
-                if j != k and not kn >> j & 1:
+            for j in sorted(deps[k], reverse=True):
+                if not kn >> j & 1:
                     mine.append(j)
                     kn |= at_issue[j] | 1 << j
             known[eng] = kn
@@ -118,7 +166,8 @@ def emit(g, T, ops):
         if ops[j][4] == "c":
             team.setdefault(tuple(waiters[j]), []).append(j)
     signal, last, count, ndma, tail, sent = {}, [0] * NPOOL, [0] * NPOOL, 0, [], 0
-    for k, (eng, fn, rd, wr, kind) in enumerate(ops):
+    for k, op in enumerate(ops):
+        eng, fn, kind = op[0], op[1], op[4]
         q = queue.get(eng)
         if kind == "arrive":
             signal[k] = fn
@@ -182,34 +231,50 @@ def rank_program(g, core, T, topo):
     def by(win, off):
         return ("@", win, off)
 
-    def copy(out, src):
-        if out[0] == "@":
-            ops.append(("v", lambda q: q.tensor_copy(ap(out), ap(src)), parts(src, out[2]), [out[1]], "c"))
+    def size(v):
+        return 16 * size(v[2]) if v[0] == "@" else len(range(v[1], v[2], v[3]))
+
+    def ns(out, a, *more, rate=1.0):
+        if out[0] == "@" or a[0] == "@":
+            return 55.0 + size(a) * (3.2 if out[0] == "@" else 1.3)
+        if all(SCRATCH[v[0]][2] in (B, U) for v in parts(out, a, *more)):
+            rate /= 2
+        return 0.83 * max(64.0, size(a) * rate)
+
+    def put(eng, fn, rd, wr, t, kind="c", boost=0.0):
+        ops.append((eng, fn, rd, wr, kind, t, boost))
+
+    def copy(out, src, eng="v"):
+        if eng == "a":
+            act(out, src)
+        elif out[0] == "@":
+            put("v", lambda q: q.tensor_copy(ap(out), ap(src)), parts(src, out[2]), [out[1]], ns(out, src))
         elif SCRATCH[out[0]][2] == X4:
-            ops.append(("v", lambda q: q.tensor_copy(ap(out).bitcast(dt.uint32), ap(src)), parts(src), [out], "c"))
+            put("v", lambda q: q.tensor_copy(ap(out).bitcast(dt.uint32), ap(src)), parts(src), [out], ns(out, src))
         else:
-            ops.append(("v", lambda q: q.tensor_copy(ap(out), ap(src)), parts(src), [out], "c"))
+            put("v", lambda q: q.tensor_copy(ap(out), ap(src)), parts(src), [out], ns(out, src))
 
     def ts(out, a, s1, o1, s2=None, o2=None):
         if o2 is None:
-            ops.append(("v", lambda q: q.tensor_scalar(ap(out), ap(a), arg(s1), None, o1), parts(a, s1), [out], "c"))
+            put("v", lambda q: q.tensor_scalar(ap(out), ap(a), arg(s1), None, o1), parts(a, s1), [out], ns(out, a, s1))
         else:
-            ops.append(("v", lambda q: q.tensor_scalar(ap(out), ap(a), arg(s1), arg(s2), o1, o2), parts(a, s1, s2), [out], "c"))
+            put("v", lambda q: q.tensor_scalar(ap(out), ap(a), arg(s1), arg(s2), o1, o2), parts(a, s1, s2), [out], ns(out, a, s1, s2))
 
     def tt(out, a, b, o):
-        ops.append(("v", lambda q: q.tensor_tensor(ap(out), ap(a), ap(b), o), parts(a, b), [out], "c"))
+        both = a[0] != "@" and SCRATCH[a[0]][0] == "sbuf"
+        put("v", lambda q: q.tensor_tensor(ap(out), ap(a), ap(b), o), parts(a, b), [out], ns(out, a, b, rate=2.0 if both else 1.0))
 
     def scan(out, d0, d1, init, o0, o1):
-        ops.append(("v", lambda q: q.tensor_tensor_scan(ap(out), ap(d0), ap(d1), init, o0, o1), parts(d0, d1), [out], "c"))
+        put("v", lambda q: q.tensor_tensor_scan(ap(out), ap(d0), ap(d1), arg(init), o0, o1), parts(d0, d1, init), [out], ns(out, d0, d1))
 
     def turn(out, a):
-        ops.append(("v", lambda q: q.transpose(ap(out), ap(a)), [a], [out], "c"))
+        put("v", lambda q: q.transpose(ap(out), ap(a)), [a], [out], ns(out, a))
 
     def fill(out, c):
-        ops.append(("v", lambda q: q.memset(ap(out), c), [], [out], "c"))
+        put("v", lambda q: q.memset(ap(out), c), [], [out], ns(out, out))
 
-    def quant(q_, s_, a):
-        ops.append(("v", lambda q: q.quantize_mx(ap(q_), ap(s_), ap(a)), [a], [q_, s_], "c"))
+    def quant(q_, s_, a, boost=0.0):
+        put("v", lambda q: q.quantize_mx(ap(q_), ap(s_), ap(a)), [a], [q_, s_], 12.0 + 0.22 * size(a), boost=boost)
 
     def act(out, a, func=ACT.Copy, scale=None, bias=None, acc=None):
         kw = {}
@@ -219,31 +284,42 @@ def rank_program(g, core, T, topo):
             kw["bias"] = arg(bias)
         if acc is not None:
             kw["accum_out"] = ap(acc)
-        ops.append(("a", lambda q: q.activation(ap(out), ap(a), func, **kw), parts(a, scale, bias), parts(out, acc), "c"))
+        t = 65.0 + 1.3 * size(a) if a[0] == "@" else 0.83 * max(64, size(a)) + (20.0 if acc else 0.0)
+        put("a", lambda q: q.activation(ap(out), ap(a), func, **kw), parts(a, scale, bias), parts(out, acc), t)
 
     def mm(out, wq, wsc, xq, xsc):
-        ops.append(("p", lambda q: q.matmul_mx(ap(out), ap(wq), ap(wsc), ap(xq), ap(xsc), True, True), [wq, wsc, xq, xsc], [out], "c"))
+        put("p", lambda q: q.matmul_mx(ap(out), ap(wq), ap(wsc), ap(xq), ap(xsc), True, True), [wq, wsc, xq, xsc], [out], 60.0)
 
     def iota(out, pattern, base=0, cm=0):
+        t = 130.0 + 1.66 * size(out)
         if SCRATCH[out[0]][2] == I:
-            ops.append(("g", lambda q: q.iota(ap(out), pattern, base, cm), [], [out], "c"))
+            put("g", lambda q: q.iota(ap(out), pattern, base, cm), [], [out], t)
         else:
-            ops.append(("g", lambda q: q.iota(ap(out), pattern, base, cm, allow_small_or_imprecise_dtypes=True), [], [out], "c"))
+            put("g", lambda q: q.iota(ap(out), pattern, base, cm, allow_small_or_imprecise_dtypes=True), [], [out], t)
 
-    def first_zero(out, n, w):
-        one = V("one", 0, n * w)
-        ops.append(("g", lambda q: q.affine_select(ap(out), ap(one), [[0, n], [1, w]], A.is_gt, 0.0, 0, 0), [one], [out], "c"))
+    def zero(out):
+        iota(out, [[0, size(out)]])
+
+    def heads(out, src, n, w, c):
+        put("g", lambda q: q.affine_select(ap(out), ap(src), [[0, n], [1, w]], A.is_gt, c, 0, 0), [src], [out], 170.0 + 1.66 * n * w)
 
     def dma(eng, out, src, rd, wr):
-        ops.append((eng, lambda q: q.dma_start(out, src), rd, wr, "dma"))
+        put(eng, lambda q: q.dma_start(out, src), rd, wr, 50.0, "dma")
 
     def col(k):
         return V("col", k, k + 1)
 
-    def ends(name, n, w):
-        return V(name, w - 1, n * w, w)
+    def ends(name, n, w, lo=0):
+        return V(name, lo * w + w - 1, n * w, w)
 
-    cA, cH, cQ, cJ, cA4, cT, cE, c6A, c32, cS4, cS16, cS1, c2A, cTH = range(14)
+    def gather(out, win, lst, share):
+        n = PART[lst][2]
+        cut = 2 * int(n * share / 2 + 0.5)
+        for eng, a, b in (("v", 0, cut), ("a", cut, n)):
+            if b > a:
+                copy(V(out, 16 * a, 16 * b), by(win, V(lst, a, b)), eng)
+
+    cH, cE, cA, cJ, cA4, cT, cS4, cS16, cS1, c2A, cTH, cU, cU4, cN, cN2, cX, cY, cA1 = range(18)
 
     dma("s", ap(V("X", 0, 768)), T.x[:, :], [], [V("X", 0, 768)])
     dma("s", ap(V("qw")).bitcast(dt.uint8), T.wc[:, :], [], [V("qw")])
@@ -251,316 +327,251 @@ def rank_program(g, core, T, topo):
     dma("s", ap(V("vt")), T.v[:, :], [], [V("vt")])
 
     iota(V("ip", 0, 1), [[0, 1]], 0, 1)
-    iota(V("qq"), [[0, 3], [1, 4], [0, 2]])
+    iota(V("ip", 1, 2), [[0, 1]], 127, -1)
+    iota(V("iu"), [[0, 3], [4096, 4], [0, 2]], 128 * 127 + 4096, -127)
     iota(V("rl"), [[32, 3], [0, 4], [16, 2]])
-    iota(V("k16"), [[0, 7], [1, 16]])
+    iota(V("k16"), [[0, 6], [1, 16]])
     iota(V("irep", 0, 6), [[32, 6]], 31)
     iota(V("irep", 6, 12), [[4, 6]], 3)
-    iota(V("u6"), [[1, 6]])
-    iota(V("n4"), [[128, 2]], 31)
-    iota(V("k6"), [[1, 16], [0, 6]])
-    iota(V("k4"), [[0, 25], [1, 4]])
+    iota(V("irep", 12, 18), [[32, 3], [H, 2]], 31)
+    iota(V("irep", 18, 24), [[16, 6]], 15)
+    iota(V("n4"), [[64, 2]], 31)
+    iota(V("k4"), [[0, 48], [1, 4]])
     iota(V("k32"), [[0, 2], [1, 32]])
-    iota(V("one"), [[0, 192]], 1)
-    first_zero(V("r32"), 6, 32)
-    first_zero(V("r16"), 6, 16)
-    iota(V("vals"), [[H, 2], [1, 6], [CH, 16]])
+    iota(V("k2"), [[1, 32], [0, 2]])
+    fill(V("one"), 1.0)
+    fill(V("big"), HUGE)
+    heads(V("t32"), V("big"), 6, 32, TINY)
+    heads(V("r32"), V("one"), 3, 32, 0.0)
+    heads(V("r16"), V("one"), 6, 16, 0.0)
+    heads(V("r16b"), V("one"), 6, 16, 0.0)
+    iota(V("vals"), [[1, C]])
     iota(V("ka4"), [[0, 6], [1, 4], [0, 4]])
-    iota(V("base"), [[32, 24], [0, 4]])
-    iota(V("th"), [[0, 32]])
-    iota(V("a0", 0, 768, 2), [[0, 384]])
-    iota(V("r4"), [[0, 8], [256, 4]])
-    iota(V("zt"), [[0, 512]])
+    iota(V("base"), [[8, 24], [0, 4]])
+    iota(V("r4"), [[0, 8], [64, 4]])
+    for v in (V("th", 24, 32), V("cz", 0, C, 2), V("zt"), V("SX", 768, 776), V("AR", 768, 776), V("Mt", 384, 512)):
+        zero(v)
 
     def same(out, a, c):
         act(out, a, ACT.Abs, scale=-1.0, bias=c)
         act(out, out, ACT.Relu, scale=-1.0, bias=1.0)
 
+    def radix(out, k, tmp, c):
+        act(tmp, k, ACT.Sign, bias=c)
+        act(tmp, tmp, ACT.Abs, scale=RADIX + 1.0, bias=col(cX))
+        act(out, tmp, ACT.Abs, bias=col(cY))
+
     fill(V("X", 768, 896), 0.0)
-    fill(V("At", 384, 512), 0.0)
-    for k, (sh, m) in enumerate([(0, 15), (4, 1), (5, 3), (0, 31), (2, 3), (0, 3)]):
-        ts(V("ic", k, k + 1), V("ip", 0, 1), sh, A.logical_shift_right, m, A.bitwise_and)
-    fill(V("Rt", 384, 512), 0.0)
-    copy(V("col", 0, 6), V("ic"))
-    fill(V("Mt", 384, 512), 0.0)
-    ts(col(cE), col(cH), -1.0, A.mult, 1.0, A.add)
-    ts(V("qq"), V("qq"), col(cQ), A.not_equal, 1000.0, A.mult)
-    copy(V("colb", 1, 2), col(cH))
-    copy(V("colb", 0, 1), col(cE))
-    tt(V("rl"), V("rl"), V("qq"), A.add)
-    act(col(c6A), col(cA), scale=float(CH))
-    act(col(c32), col(cA4), scale=32.0)
+    fill(col(cX), 0.5)
+    fill(col(cY), -RADIX - 0.5)
+    ts(V("ic", 0, 2), V("ip"), 4, A.logical_shift_right, 1, A.bitwise_and)
+    copy(V("colb"), V("ic", 0, 2))
+    copy(V("col", 0, 2), V("ic", 0, 2))
+    for k, (sh, m) in enumerate([(0, 15), (0, 31), (2, 3), (0, 3)]):
+        ts(V("ic", 2 + k, 3 + k), V("ip", 0, 1), sh, A.logical_shift_right, m, A.bitwise_and)
+    copy(V("col", 2, 6), V("ic", 2, 6))
+    ts(V("iw"), V("iu"), 3 * 4096 + 15, A.bitwise_and)
+    tt(V("rq"), V("iw"), V("rl"), A.add)
+    ts(V("op2"), V("rq"), float(C), A.min)
+    ts(V("op1"), V("rq"), float(H), A.min)
+    ts(V("op3"), V("rq"), float(H), A.min, 2.0, A.mult)
+    ts(V("opf"), V("rq"), float(H), A.min, 2.0, A.mult)
+    ts(V("op4"), V("opf"), 1.0, A.add)
+    ts(col(cN2), col(cA4), 2.0, A.is_ge, 32.0 - C, A.mult)
+    act(col(cN), col(cA4), ACT.Identity, scale=float(H), bias=col(cN2))
+    ts(V("on4"), V("n4"), col(cN), A.add, float(C - 1), A.min)
     ts(col(cS1), col(cA4), 3.0, A.is_equal, 1.0 / RADIX, A.max)
-    ts(V("op2"), V("rl"), col(cA), A.add, float(C), A.min)
-    ts(V("op1"), V("rl"), col(cA), A.add, float(H), A.min)
     ts(col(cS16), col(cA), 15.0, A.is_equal, 1.0 / RADIX, A.max)
+    act(col(cU), col(cA), ACT.Identity, scale=-1.0, bias=-1.0)
+    act(col(cU4), col(cA4), ACT.Identity, scale=-1.0, bias=-1.0)
+    act(col(cA1), col(cA), ACT.Identity, bias=-0.5)
     same(V("d16"), V("k16"), col(cA))
-    act(V("g16"), V("d16", 15, 111), ACT.Identity, scale=RADIX - 1.0, bias=1.0)
+    same(V("eye"), V("k32"), col(cJ))
+    same(V("eye2"), V("k2"), col(cJ))
+    radix(V("g16"), V("k16"), V("s16"), col(cU))
+    radix(V("g4"), V("k4"), V("k4"), col(cU4))
     copy(V("orep"), V("irep"))
-    ts(V("oown"), V("u6"), col(c6A), A.add)
-    ts(V("on4"), V("n4"), col(c32), A.add, float(C - 1), A.min)
-    ts(V("m6"), V("k6"), col(cA), A.is_lt, BELOW - 1.0, A.mult)
-    ts(V("mul"), V("k6"), col(cA), A.not_equal)
+    act(V("mul"), V("k16"), ACT.Sign, scale=-1.0, bias=col(cA1))
+    act(V("mul"), V("mul"), ACT.Relu, scale=1.0 - BELOW)
+    act(V("mul"), V("mul"), ACT.Identity, scale=-1.0, bias=1.0)
+    act(col(cS4), col(cS1), scale=4.0)
+    act(col(c2A), col(cA4), scale=2.0)
+    act(col(cTH), col(cT), scale=HUGE)
+    act(V("ka4"), V("ka4"), ACT.Abs, scale=-HUGE, bias=col(cTH))
+    act(V("base"), V("base"), ACT.Identity, bias=col(c2A))
+    act(V("b2"), ends("base", 24, 4), ACT.Identity, scale=2.0, bias=1.0)
 
-    def later_b():
-        same(V("d4"), V("k4"), col(cA4))
-        act(V("g4"), V("d4", 3, 99), ACT.Identity, scale=RADIX - 1.0, bias=1.0)
-        act(col(cS4), col(cS1), scale=4.0)
-        act(col(c2A), col(cA), scale=2.0)
-        act(col(cTH), col(cT), scale=HUGE)
+    REP, CREP, REP2, REP16 = (V("orep", k, k + 6) for k in (0, 6, 12, 18))
+    PK, PG = ["pk0", "pk1", "pk2"], ["pg0", "pg1", "pg2"]
 
-    def later_c():
-        act(V("ka4"), V("ka4"), ACT.Abs, scale=-HUGE, bias=col(cTH))
-        act(V("base"), V("base"), ACT.Identity, bias=col(c2A))
-        act(V("b2"), ends("base", 24, 4), ACT.Identity, scale=2.0, bias=1.0)
+    def mask(out, src, h, eng):
+        if eng == "a":
+            act(out, src, scale=col(cE if h == 0 else cH))
+        else:
+            ts(out, src, V("colb", 1 - h, 2 - h), A.mult)
 
-    REP, CREP = V("orep", 0, 6), V("orep", 6, 12)
-
-    def masks(src, gm, which, eng):
-        for b, h in which:
-            out = V(gm, 256 * b + 128 * h, 256 * b + 128 * h + 128)
-            if eng == "a":
-                act(out, src(b), scale=col(cE if h == 0 else cH))
-            else:
-                ts(out, src(b), V("colb", h, h + 1), A.mult)
-
-    PAIRS = [(b, h) for b in range(3) for h in range(2)]
-
-    def picks(k, qwin, lst, b, e):
-        copy(V("qs%d" % k, 128 * b, 128 * e), by(qwin, V(lst, 8 * b, 8 * e)))
-
-    def spicks(k, swin, lst, b, e):
-        act(V("ss%d" % k, 128 * b, 128 * e), by(swin, V(lst, 8 * b, 8 * e)))
-
-    def products(k, qg, sg, banks):
+    def products(k, kind, qf, sf, lst, banks, eye):
+        quant(V("qg" + kind), V("sg" + kind), V("G" + kind), Z["boost"])
+        for b, e in ((0, 2), (2, 3)):
+            copy(V("qs%d" % k, 128 * b, 128 * e), by(qf, V(lst, 8 * b, 8 * e)))
+            act(V("ss%d" % k, 128 * b, 128 * e), by(sf, V(lst, 8 * b, 8 * e)))
         for b in range(3):
             lo = min(64 * b, 64)
             mm(V(banks[b], 0, 128), V("qs%d" % k, 128 * b, 128 * b + 128), V("ss%d" % k, 128 * b, 128 * b + 128),
-               V(qg, lo, lo + 128), V(sg, lo, lo + 128))
+               V("qg" + kind, lo, lo + 128), V("sg" + kind, lo, lo + 128))
+            tt(V("D" + kind, 64 * b, 64 * b + 64), V(banks[b], 64 * b - lo, 64 * b - lo + 64), V(eye), A.mult)
 
-    def diagonals(banks):
-        for b in range(3):
-            lo = 64 * b - min(64 * b, 64)
-            tt(V("D", 64 * b, 64 * b + 64), V(banks[b], lo, lo + 64), V("eye"), A.mult)
+    def sizes(k, kind, lo, qf, sf, lst, banks, nact):
+        for n, (b, h) in enumerate([(b, h) for b in range(3) for h in range(2)]):
+            mask(V("G" + kind, 256 * b + 128 * h, 256 * b + 128 * h + 128), V("X", lo + 128 * b, lo + 128 * b + 128), h, "a" if n < nact else "v")
+        products(k, kind, qf, sf, lst, banks, "eye")
+        for a, e in ((0, 128), (128, C)):
+            scan(V("E" + kind, a, e), V("t32", a, e), V("D" + kind, a, e), 1.0, A.min, A.add)
+        tt(V("prw" + kind), by(V("E" + kind), REP), V("d16"), A.mult)
+        copy(V("pre" + kind), by(V("E" + kind), REP), Z["pre"])
 
-    def sums(lo=0, hi=192):
-        scan(V("E", lo, hi), V("r32", lo, hi), V("D", lo, hi), 0.0, A.mult, A.add)
-
-    PG = ["pg0", "pg1", "pg2"]
-
-    def extract():
-        diagonals(PG)
-        sums(0, 128)
-        sums(128, 192)
-
-    def gram(k, full, src, gap=None):
+    def paired(k, kind, name, lst, banks, nact):
         qf, sf = V("qf%d" % k), V("sf%d" % k)
-        masks(src, "Gm", PAIRS[6 - ACT_MASKS:], "a")
-        if gap:
-            masks(src, "Gm", PAIRS[:6 - ACT_MASKS], "v")
-            quant(qf, sf, full)
-            quant(V("qg"), V("sg"), V("Gm"))
-            picks(k, qf, "op1", 0, 2)
+        quant(qf, sf, V(name))
+        for n, (e, h) in enumerate([(e, h) for e in range(4) for h in range(2)]):
+            mask(V("G" + kind, 4 * h + e, 768, 8), V(name, 4 + e, 768, 8), h, "a" if n < nact else "v")
+        products(k, kind, qf, sf, lst, banks, "eye2")
+        for a, e in ((0, 64), (64, H)):
+            for h in range(2):
+                out, d = V("E" + kind, H * h + a, H * h + e), V("D" + kind, 2 * a + h, 2 * e, 2)
+                if kind == "A":
+                    scan(out, V("r32", a, e), d, 0.0, A.mult, A.add)
+                else:
+                    scan(out, V("t32", a, e), d, 1.0, A.min, A.add)
+
+    def spread(kind, lo):
+        turn(V("own" + kind), V("prw" + kind))
+        turn(V("row", lo, lo + H), V("pre" + kind))
+        scan(V("ow" + kind), V("r16"), V("own" + kind), 0.0, A.mult, A.add)
+        tt(V("mix" + kind), V("row", lo, lo + H), V("mul"), A.mult)
+        tt(V("fm" + kind), by(V("ow" + kind), REP16), V("mix" + kind), A.is_gt)
+        scan(V("in" + kind), V("r16b"), V("fm" + kind), 0.0, A.mult, A.add)
+
+    def count(on_act, w, o, signs, flags, res, more):
+        n = size(w)
+        name, at = res
+        if on_act:
+            act(V(signs[0], signs[1], signs[1] + n), w, ACT.Sign, scale=-1.0, bias=o)
+            s = V(signs[0], signs[1], signs[1] + n + 1)
+            act(s, s, ACT.Relu, acc=V(name, at, at + 1))
         else:
-            quant(qf, sf, full)
-            masks(src, "Gm", PAIRS[:6 - ACT_MASKS], "v")
-            picks(k, qf, "op1", 0, 2)
-            quant(V("qg"), V("sg"), V("Gm"))
-        picks(k, qf, "op1", 2, 3)
-        spicks(k, sf, "op1", 0, 2)
-        spicks(k, sf, "op1", 2, 3)
-        products(k, "qg", "sg", PG)
-        if gap:
-            gap()
-        extract()
+            ts(V(flags[0], flags[1], flags[1] + n), w, o, A.is_lt)
+            scan(V(name, at + 1 - n // 2, at + 1), V(flags[0], flags[1], flags[1] + n // 2), V(flags[0], flags[1] + n // 2, flags[1] + n),
+                 more, A.add, A.add)
 
-    def spread():
-        ts(V("pre"), by(V("E"), REP), TINY, A.max)
+    def end16(name, m):
+        return V(name, 16 * m + 15, 16 * m + 16)
 
-    def own_sizes(lo):
-        tt(V("own"), by(V("row", lo, lo + H), V("oown")), V("d16", 16, 112), A.mult)
+    def old_half(nact):
+        spread("S", 0)
+        act(V("cs", 0, WS), V("row", 16, H))
+        act(V("cs", WS, 2 * WS), V("row", 0, WS), scale=BELOW)
+        act(V("row", C, C + H), V("row", 0, H), scale=BELOW)
+        if nact:
+            act(ends("snS", nact, WS + 1), ends("inS", nact, 16))
+        for m in range(CH):
+            count(m < nact, V("cs", 16 * m, 16 * m + WS), end16("owS", m), ("snS", (WS + 1) * m), ("fs", WS * m),
+                  ("sn", (H + 1) * m + H), end16("inS", m))
 
-    def window(buf, lo, tail, scratch, picked=False):
-        if not picked:
-            own_sizes(lo)
-            tt(V(buf, CH, CH + H), V("row", lo, lo + H), V("mul"), A.mult)
-            scan(V(scratch), V("r16"), V("own"), 0.0, A.mult, A.add)
-        copy(V(buf, 0, CH), ends(scratch, CH, 16))
-        ts(V(buf, tail, tail + CH), ends(scratch, CH, 16), BELOW, A.mult)
+    def new_half(nsk, nkk):
+        spread("K", H)
+        act(V("row", C + H, C + H + WS), V("row", H, H + WS), scale=BELOW)
+        for m in range(CH):
+            at = (H + 1) * m
+            count(m < nsk, V("row", H, C), end16("owS", m), ("sn", at), ("fx", H * m), ("fin", SLOT * m + SLOT - 1), V("sn", at + H, at + H + 1))
+        if nkk:
+            act(ends("snK", nkk, WK + 1), ends("inK", nkk, 16))
+        for m in range(CH):
+            res = ("fin", SLOT * (CH + m) + SLOT - 1) if m < nkk else ("cn", SLOT * m + SLOT - 1)
+            lo = H + 16 + 16 * m
+            count(m < nkk, V("row", lo, lo + WK), end16("owK", m), ("snK", (WK + 1) * m), ("fk", WK * m), res, end16("inK", m))
+        if Z["split"]:
+            copy(V("ork", 0, CH), ends("fin", CH, SLOT))
+            copy(by(V("O"), V("ork", 0, CH)), V("vals", 0, H))
+            if nkk:
+                copy(V("ork", CH, CH + nkk), ends("fin", CH + nkk, SLOT, CH))
+        else:
+            copy(V("ork", 0, CH + nkk), ends("fin", CH + nkk, SLOT))
+        copy(V("ork", CH + nkk, 12), ends("cn", CH, SLOT, nkk))
+        if Z["split"]:
+            copy(by(V("O"), V("ork", CH, 12)), V("vals", H, C))
+        else:
+            copy(by(V("O"), V("ork")), V("vals"))
 
-    def count_act(items):
-        for w, o, lo, n, c in items:
-            act(V("sn", lo, lo + w[2] - w[1]), w, ACT.Sign, scale=-1.0, bias=o)
-        for w, o, lo, n, c in items:
-            act(V("jk", lo, lo + n), V("sn", lo, lo + n), ACT.Relu, acc=V("cnt", c, c + 1))
+    quant(V("qf0"), V("sf0"), V("X"))
+    sizes(0, "S", 0, V("qf0"), V("sf0"), "op2", PK, Z["mk0"] // 2)
+    sizes(1, "K", 384, V("qf0", 96, 224), V("sf0", 96, 224), "op1", PG, Z["mk0"] - Z["mk0"] // 2)
+    old_half(Z["ss0"])
 
-    def count_dve(items, width):
-        h = width // 2
-
-        def total(k):
-            scan(V("cn", h * k, h * k + h), V("cb", width * k, width * k + h), V("cb", width * k + h, width * k + width), 0.0, A.add, A.add)
-
-        for k, (w, o) in enumerate(items):
-            ts(V("cb", width * k, width * k + width), w, o, A.is_lt)
-            if k > 1:
-                total(k - 2)
-        total(len(items) - 2)
-        total(len(items) - 1)
-
-    def item(buf, m, width):
-        return V(buf, m, m + width), V(buf, m, m + 1)
-
-    def xblock(lo):
-        return lambda b: V("X", lo + 128 * b, lo + 128 * b + 128)
-
-    ng = [2]
     for t in range(R):
-        if t == 0:
-            masks(xblock(0), "Gm", PAIRS[6 - ACT_MASKS:], "a")
-            quant(V("qf0"), V("sf0"), V("X"))
-            masks(xblock(0), "Gm", PAIRS[:6 - ACT_MASKS], "v")
-            masks(xblock(384), "Gm2", PAIRS[:3], "v")
-            quant(V("qg"), V("sg"), V("Gm"))
-            picks(0, V("qf0"), "op2", 0, 3)
-            spicks(0, V("sf0"), "op2", 0, 3)
-            masks(xblock(384), "Gm2", PAIRS[3:], "a")
-            same(V("eye"), V("k32"), col(cJ))
-            products(0, "qg", "sg", ["pk0", "pk1", "pk2"])
-            picks(1, V("qf0", 96, 224), "op1", 0, 3)
-            quant(V("qg2"), V("sg2"), V("Gm2"))
-            spicks(1, V("sf0", 96, 224), "op1", 0, 3)
-            products(1, "qg2", "sg2", PG)
-            later_b()
-            diagonals(["pk0", "pk1", "pk2"])
-            sums()
-            tt(V("mul"), V("mul"), V("m6"), A.add)
-            spread()
-            diagonals(PG)
-            turn(V("row", 0, H), V("pre"))
-            sums()
-            act(V("ck", WS, WS + H), V("row", 0, H), scale=BELOW)
-            own_sizes(0)
-            spread()
-            scan(V("ows"), V("r16"), V("own"), 0.0, A.mult, A.add)
-            turn(V("row", H, C), V("pre"))
-            tt(V("cs", CH, CH + H), V("row", 0, H), V("mul"), A.mult)
-            act(V("cs", WS, WS + H), V("row", H, C))
-            window("cs", 0, WK, "ows", True)
-            na = ACT_ITEMS0
-            count_act([item("cs", m, WK) + (WK * m, WK, m) for m in range(na)])
-            window("ck", H, WK, "la")
-            tt(V("g4"), V("g4"), V("d4", 4, 100), A.subtract)
-            count_dve([item("cs", m, WK) for m in range(na, CH)] + [item("ck", m, WK) for m in range(CH)], WK)
-            tt(V("g16"), V("g16"), V("d16", 16, 112), A.subtract)
-            later_c()
-        else:
-            gram(ng[0], V("X", 384, 896), xblock(384))
-            ng[0] += 1
-            spread()
-            turn(V("row", H, C), V("pre"))
-            na = CH + ACT_K
-            count_act([(V("row", H, C), V("cs", m, m + 1), (H + 1) * m, H + 1, m) for m in range(CH)])
-            window("ck", H, WK, "la")
-            count_act([item("ck", m, WK) + (CH * (H + 1) + WK * m, WK, CH + m) for m in range(ACT_K)])
-            count_dve([item("ck", m, WK) for m in range(ACT_K, CH)], WK)
-        ts(V("ork", 0, na), V("cnt", 0, na), -float(CH), A.add)
-        ts(V("ork", na, 12), ends("cn", 12 - na, WK // 2), -float(CH), A.add)
-        copy(by(V("O"), V("ork")), V("vals"))
-
-        k = ng[0]
-        ng[0] += 1
-        qf, sf = V("qf%d" % k), V("sf%d" % k)
-        scan(V("lb"), V("g4"), V("O", 1, C, 2), 0.0, A.mult, A.add)
-        scan(V("la"), V("g4"), V("O", 0, C, 2), 0.0, A.mult, A.add)
-        ts(V("ob"), ends("lb", 24, 4), col(cS4), A.mult, col(cT), A.add)
-        ts(V("oa"), ends("la", 24, 4), col(cS4), A.mult, col(cT), A.add)
-        act(V("bc", 1, 768, 2), by(V("X", 0, 768), V("ob")))
+        stage = 2 + 3 * t
+        new_half(Z["sk" if t else "sk0"], Z["kk" if t else "kk0"])
+        scan(V("lx"), V("g4"), V("O"), 0.0, A.mult, A.add)
         scan(V("ld"), V("g16"), V("O", 0, C, 2), 0.0, A.mult, A.add)
-        copy(V("At", 0, 384), by(V("X", 0, 768), V("oa")))
-        if t == R - 1:
-            dma("s", T.ol[:, :], T.O[0:128:16, :], [V("O")], [])
-        bblock = lambda b: V("bc", 256 * b + 1, 256 * b + 256, 2)
+        ts(V("ox"), ends("lx", 48, 4), col(cS4), A.mult, col(cT), A.add)
         ts(V("od"), ends("ld", CH, 16), col(cS16), A.mult)
-        quant(qf, sf, V("At"))
-        masks(bblock, "Gm", PAIRS[:6 - ACT_MASKS], "v")
-        masks(bblock, "Gm", PAIRS[6 - ACT_MASKS:], "a")
-        picks(k, qf, "op1", 0, 2)
-        act(V("da"), by(V("row"), V("od")))
-        spicks(k, sf, "op1", 0, 2)
-        spicks(k, sf, "op1", 2, 3)
-        quant(V("qg"), V("sg"), V("Gm"))
-        picks(k, qf, "op1", 2, 3)
+        gather("SX", V("X", 0, 768), "ox", Z["gx"])
+        if t == R - 1:
+            act(V("Of"), V("O"))
+            dma("s", T.ol[:, :], T.Of[0:128:16, :], [V("Of")], [])
+        act(V("da"), by(V("row", 0, C), V("od")))
         turn(V("dap"), V("da"))
         d6 = V("dap", 0, H, 16)
         act(V("th", 0, 24, 4), d6, scale=0.75)
         act(V("th", 1, 24, 4), d6, scale=0.25)
         act(V("th", 3, 24, 4), V("th", 0, 24, 4), scale=-BELOW)
         act(V("th", 2, 24, 4), V("th", 1, 24, 4), scale=-BELOW)
-        products(k, "qg", "sg", PG)
-        extract()
+        tt(V("dam"), V("dap"), V("ka4"), A.max)
+        paired(stage, "A", "SX", "op3", PK, Z["ma"])
 
-        act(V("a0", 1, 768, 2), V("At", 0, 384))
-        tt(V("cp"), by(V("E"), V("on4")), V("th"), A.is_ge)
+        tt(V("cp"), by(V("EA"), V("on4")), V("th"), A.is_ge)
         scan(V("cq"), V("r4"), V("cp"), 0.0, A.min, A.add)
         ts(V("ncp"), by(V("cq"), CREP), -0.5, A.mult, 1.0, A.add)
-        act(V("w2", 0, 768, 2), V("At", 0, 384))
+        turn(V("cz", 1, C, 2), V("ncp"))
         for e in range(4):
-            turn(V("bc", 2 * e, 768, 8), V("ncp"))
-        for lo, hi in ((0, 512), (512, 768)):
-            scan(V("ro", lo, hi), V("a0", lo, hi), V("bc", lo, hi), 0.0, A.mult, A.add)
+            scan(V("AR", e, 768, 4), V("cz"), V("SX", e, 768, 4), 0.0, A.mult, A.add)
 
-        for lo, hi in ((0, 512), (512, 768)):
-            copy(V("Rt", lo // 2, hi // 2), V("ro", lo + 1, hi, 2))
-
-        def gap():
-            act(V("w2", 1, 768, 2), V("Rt", 0, 384))
-            tt(V("dam"), V("dap"), V("ka4"), A.max)
-
-        gram(ng[0], V("Rt"), lambda b: V("ro", 256 * b + 1, 256 * b + 256, 2), gap)
-        ng[0] += 1
-        tt(V("swp"), by(V("E"), REP), V("dam"), A.is_ge)
+        paired(stage + 1, "R", "AR", "op4", PG, Z["mr"])
+        tt(V("swp"), by(V("ER"), REP2), V("dam"), A.is_ge)
         turn(V("swr"), V("swp"))
         scan(V("lm"), V("base"), V("swr"), 0.0, A.max, A.add)
-        copy(V("om"), ends("lm", 24, 4))
-        copy(V("Mt", 0, 192), by(V("w2"), V("om", 0, 12)))
-        act(V("Mt", 192, 384), by(V("w2"), V("om", 12, 24)))
+        ts(V("om"), ends("lm", 24, 4), 4.0, A.mult, col(cT), A.add)
+        gather("Mt", V("AR", 0, 768), "om", Z["gm"])
         qm, sm = "qm%d" % t, "sm%d" % t
         quant(V(qm), V(sm), V("Mt"))
         dst = T.cores[(rank + STEP[t]) % N]
+        src = T.cores[(rank - STEP[t]) % N]
         rid, pid = topo.addr(dst, core)
-        mask = topo.mask(core, dst)
+        engines = topo.mask(core, dst)
         neng = len(topo.engines(core, dst))
-        lo = 128 + H * t
+        at = 128 + H * t
         arr = T.sem["arr%d" % t]
 
-        def send(out, src, arr=arr, rid=rid, pid=pid, mask=mask, neng=neng):
+        def send(out, src, arr=arr, rid=rid, pid=pid, engines=engines, neng=neng):
             def go(q):
-                q.remote_dma(out, src, arr, T.sem.sent, pid, rid, mask)
+                q.remote_dma(out, src, arr, T.sem.sent, pid, rid, engines)
                 return neng
             return go
 
-        ops.append(("g", send(ap(V("ql", lo, lo + H)).bitcast(dt.uint8), ap(V(qm, 0, H)).bitcast(dt.uint8)), [V(qm, 0, H)], [], "remote"))
-        ops.append(("g", send(ap(V("sl", lo, lo + H)), ap(V(sm, 0, H))), [V(sm, 0, H)], [], "remote"))
-        src = T.cores[(rank - STEP[t]) % N]
-        ops.append(("x", (arr, 2 * len(topo.engines(src, core))), [], [V("ql", lo, lo + H), V("sl", lo, lo + H)], "arrive"))
+        lq, ls = V("ql", at, at + H), V("sl", at, at + H)
+        put("g", send(ap(lq).bitcast(dt.uint8), ap(V(qm, 0, H)).bitcast(dt.uint8)), [V(qm, 0, H)], [], 100.0, "remote")
+        put("g", send(ap(ls), ap(V(sm, 0, H))), [V(sm, 0, H)], [], 100.0, "remote")
+        put("x", (arr, 2 * len(topo.engines(src, core))), [V(qm, 0, H)], [lq, ls], Z["send"], "arrive")
 
         tt(V("ls"), V("b2"), ends("lm", 24, 4), A.subtract)
-        if t < R - 1:
-            tt(V("pre"), by(V("E"), REP), V("dap"), A.min)
-        copy(V("oz"), V("ls"))
+        ts(V("oz"), V("ls"), 4.0, A.mult, col(cT), A.add)
+        gather("X", V("AR", 0, 768), "oz", 0.0)
         if t == 0:
             quant(V("ql", 0, 128), V("sl", 0, 128), V("zt"))
-        act(V("X", 0, 384), by(V("w2"), V("oz")))
         if t < R - 1:
-            ts(V("pre"), V("pre"), TINY, A.max)
-            turn(V("row", 0, H), V("pre"))
-            act(V("ck", WS, WS + H), V("row", 0, H), scale=BELOW)
-            window("cs", 0, WS, "ows")
-            at = CH * (H + 1) + WK * ACT_K
-            count_act([item("cs", m, WS) + (at + WS * m, WS, 12 + m) for m in range(ACT_S)])
-            act(V("sn", H, ACT_S * (H + 1), H + 1), V("cnt", 12, 12 + ACT_S))
-            count_dve([item("cs", m, WS) for m in range(ACT_S, CH)], WS)
-            copy(V("sn", ACT_S * (H + 1) + H, CH * (H + 1), H + 1), ends("cn", CH - ACT_S, WS // 2))
+            tt(V("preS"), by(V("ER"), REP2), V("dap"), A.min)
+            tt(V("prwS"), V("preS"), V("d16"), A.mult)
+            old_half(Z["ss"])
         else:
             quant(V("qv"), V("sv"), V("vt"))
             quant(V("qxs"), V("sxs"), V("X", 0, 512))
@@ -573,10 +584,14 @@ def rank_program(g, core, T, topo):
 
         for b in (2, 0, 3, 1):
             mm(V("pk%d" % b, 0, 128), V("qw", 128 * b, 128 * b + 128), V("sw", 128 * b, 128 * b + 128),
-               V("ql", lo - 32, lo + H), V("sl", lo - 32, lo + H))
+               V("ql", at - 32, at + H), V("sl", at - 32, at + H))
         for b in (0, 1):
             ts(V("X", 384 + b, 768, 4), V("pk%d" % b, 32, 128), 0.03125, A.mult)
             act(V("X", 386 + b, 768, 4), V("pk%d" % (b + 2), 32, 128), scale=0.03125)
+        if t < R - 1:
+            qf, sf = V("qf%d" % (stage + 2), 0, 128), V("sf%d" % (stage + 2), 0, 128)
+            quant(qf, sf, V("X", 384, 896))
+            sizes(stage + 2, "K", 384, qf, sf, "op1", PG, Z["mk"])
 
     quant(V("qxk"), V("sxk"), V("X", 384, 896))
     mm(V("pg0", 0, 128), V("qv"), V("sv"), V("qxk"), V("sxk"))

@@ -1,3 +1,5 @@
+import math
+
 from concourse.mybir import dt, AluOpType, ActivationFunctionType
 
 C, H, R = 192, 96, 3
@@ -10,8 +12,8 @@ CH = 6
 WS = H - 16
 WK = WS + H
 SLOT = 100
-Z = dict(ss=3, sk=4, kk=2, ss0=2, sk0=4, kk0=2, mk=3, ma=4, mr=4, split=1, pre="a", wake=250.0, send=1500.0, load=1400.0,
-         mk0=6, gx=0.5, gm=0.5, boost=100.0)
+Z = dict(each=(8.0, 16.0), tries=70000, slack=7.0, speeds=((1.0, 1.0, 1.0, 220.0), (1.3, 0.7, 1.1, 220.0), (1.0, 0.9, 0.67, 250.0)), soon=0.002, late=-400.0, early=300.0, ss=3, sk=4, kk=2, gz=0.0, sc=6, sk0=3, kk0=2, mk=0.5, ma=5, mr=5, split=1, pre="aa", wake=215.0, send=1800.0, load=1400.0, fan=1.0, noise=lambda j: 0.0,
+         mk0=(0.34, 0.67), gx=(0.5, 0.5), gm=(0.5, 0.5), boost=100.0, pk=2, sends=(1, 1, 1), qs=dict(A=0, R=1))
 
 F, B, I, U = "float32", "bfloat16", "int32", "uint16"
 X4, U8 = "float8_e4m3fn_x4", "uint8"
@@ -22,38 +24,38 @@ def _sb(n, d):
 
 
 SCRATCH = {
-    "X": _sb(896, B), "SX": _sb(776, B), "AR": _sb(776, B), "Mt": _sb(512, B), "vt": _sb(512, B), "zt": _sb(512, B),
+    "X": _sb(896, B), "SX": _sb(776, B), "AR": _sb(1040, B), "Mt": _sb(768, B), "vt": _sb(512, B), "zt": _sb(512, B),
     "qw": _sb(512, X4), "sw": _sb(512, U8), "qv": _sb(128, X4), "sv": _sb(128, U8),
     "ql": _sb(416, X4), "sl": _sb(416, U8),
     "qxs": _sb(128, X4), "sxs": _sb(128, U8), "qxk": _sb(128, X4), "sxk": _sb(128, U8),
     "yt": _sb(192, F), "Of": _sb(192, F), "ip": _sb(2, I), "ic": _sb(8, I), "iu": _sb(24, I), "iw": _sb(24, I), "irep": _sb(24, I),
 }
 for _k in "SKAR":
-    SCRATCH["G" + _k], SCRATCH["qg" + _k], SCRATCH["sg" + _k] = _sb(768, B), _sb(192, X4), _sb(192, U8)
+    SCRATCH["G" + _k], SCRATCH["qg" + _k], SCRATCH["sg" + _k] = _sb(768 if _k in "SK" else 784, B), _sb(256, X4), _sb(256, U8)
 for _k in ("pk0", "pk1", "pk2", "pk3", "pg0", "pg1", "pg2", "py"):
     SCRATCH[_k] = ("psum", [128, 512], F)
-SCRATCH["qf0"], SCRATCH["sf0"] = _sb(224, X4), _sb(224, U8)
+SCRATCH["qf0"], SCRATCH["sf0"], SCRATCH["X0"] = _sb(256, X4), _sb(256, U8), _sb(512, B)
 for _k in range(2, 10):
-    SCRATCH["qf%d" % _k], SCRATCH["sf%d" % _k] = _sb(194, X4), _sb(194, U8)
+    SCRATCH["qf%d" % _k], SCRATCH["sf%d" % _k] = _sb(288, X4), _sb(288, U8)
 for _k in range(10):
     SCRATCH["qs%d" % _k], SCRATCH["ss%d" % _k] = _sb(384, X4), _sb(384, U8)
 for _k in range(R):
-    SCRATCH["qm%d" % _k], SCRATCH["sm%d" % _k] = _sb(128, X4), _sb(128, U8)
+    SCRATCH["qm%d" % _k], SCRATCH["sm%d" % _k] = _sb(256, X4), _sb(256, U8)
 
 PART = {}
 for _buf, _dt, _names in (
         ("cf", F, (("col", 32), ("k32", 64), ("eye", 64), ("k2", 64), ("eye2", 64), ("one", 96), ("big", 192), ("r32", 96), ("t32", 192),
-                   ("rl", 24), ("rq", 24), ("opf", 24), ("n4", 2), ("k16", 96), ("s16", 96), ("d16", 96), ("r16", 96), ("k4", 192),
+                   ("rl", 24), ("rq", 24), ("opf", 24), ("n6", 6), ("t16", 192), ("k16", 96), ("s16", 96), ("d16", 96), ("r16", 96), ("k4", 192),
                    ("mul", 96), ("ka4", 96), ("b2", 24))),
-        ("cb", B, (("colb", 2), ("r4", 32), ("g16", 96), ("g4", 192), ("base", 96), ("vals", 192), ("r16b", 96))),
-        ("cu", U, (("op1", 24), ("op2", 24), ("op3", 24), ("op4", 24), ("orep", 24), ("on4", 2))),
+        ("cb", B, (("colb", 2), ("r4", 32), ("g16", 96), ("g4", 192), ("base", 96), ("vals", 192))),
+        ("cu", U, (("op1", 24), ("op2", 24), ("op3", 24), ("op4", 24), ("orep", 24), ("on4", 4))),
         ("wf", F, (("DS", 192), ("DK", 192), ("DA", 192), ("DR", 192), ("ES", 192), ("EK", 192), ("EA", 192), ("ER", 192),
-                   ("preS", 96), ("preK", 96), ("prwS", 96), ("prwK", 96), ("row", C + H + WS), ("ownS", 96), ("ownK", 96),
-                   ("owS", 96), ("owK", 96), ("mixS", 96), ("mixK", 96), ("cs", 2 * WS), ("sn", CH * (H + 1)),
-                   ("snS", CH * (WS + 1)), ("snK", CH * (WK + 1)), ("fin", 12 * SLOT), ("inS", 96), ("inK", 96),
+                   ("preS", 96), ("preK", 96), ("prwS", 96), ("prwK", 96), ("row", C + H + WS), ("ownS", 192), ("ownK", 192),
+                   ("owS", 192), ("owK", 192), ("mixS", 96), ("mixK", 96), ("rs", H + WS), ("sn", CH * (H + 1)),
+                   ("snS", CH * H), ("snK", CH * C), ("snW", CH * C), ("fin", 12 * SLOT),
                    ("da", 96), ("dap", 96), ("dam", 96), ("th", 32), ("cq", 32), ("ls", 24))),
-        ("wb", B, (("fs", CH * WS), ("fx", CH * H), ("fk", CH * WK), ("cn", CH * SLOT), ("O", 192), ("lx", 192), ("ld", 96), ("cp", 32),
-                   ("ncp", 96), ("cz", 192), ("swp", 96), ("swr", 96), ("lm", 96), ("fmS", 96), ("fmK", 96))),
+        ("wb", B, (("fs", CH * H), ("fx", CH * H), ("fk", CH * C), ("fw", CH * C), ("cn", CH * SLOT), ("O", 192), ("lx", 192), ("ld", 96), ("cp", 32),
+                   ("ncp", 96), ("cz", 192), ("swp", 96), ("swr", 96), ("lm", 96))),
         ("wu", U, (("ork", 12), ("ox", 48), ("od", 6), ("om", 24), ("oz", 24)))):
     _at = 0
     for _n, _w in _names:
@@ -61,8 +63,8 @@ for _buf, _dt, _names in (
         _at += (_w + 15) // 16 * 16
     SCRATCH[_buf] = _sb(_at, _dt)
 
-NPOOL = 124
-SEMAPHORES = ["c%d" % k for k in range(NPOOL)] + ["d%d" % k for k in range(20)] + ["arr%d" % k for k in range(R)] + ["sent"]
+NPOOL = 123
+SEMAPHORES = ["c%d" % k for k in range(NPOOL)] + ["d%d" % k for k in range(20)] + ["arr%d" % k for k in range(2 * R)] + ["sent"]
 
 
 def V(name, lo=0, hi=None, step=1):
@@ -114,7 +116,11 @@ def arrange(ops, deps):
             after[j].append(k)
     chain = [0.0] * n
     for k in range(n - 1, -1, -1):
-        chain[k] = ops[k][5] + late[ops[k][4]] + max([Z["wake"] + chain[j] for j in after[k]], default=0.0)
+        ahead, most = {}, 0.0
+        for j in sorted(after[k], key=lambda j: ops[j][5] - chain[j]):
+            most = max(most, Z["wake"] + Z["fan"] * ahead.get(ops[j][0], 0.0) + chain[j])
+            ahead[ops[j][0]] = ahead.get(ops[j][0], 0.0) + ops[j][5]
+        chain[k] = ops[k][5] + late[ops[k][4]] + most
     left = [len(d) for d in deps]
     due = [0.0] * n
     ready = {k for k in range(n) if not left[k]}
@@ -123,7 +129,7 @@ def arrange(ops, deps):
         start = {k: max(due[k], free.get(ops[k][0], 0.0)) for k in ready}
         first = min(ready, key=lambda k: (start[k] + ops[k][5], k))
         end = start[first] + ops[first][5]
-        k = max((j for j in ready if ops[j][0] == ops[first][0] and start[j] < end), key=lambda j: (chain[j] + ops[j][6], -j))
+        k = max((j for j in ready if ops[j][0] == ops[first][0] and start[j] < end), key=lambda j: (chain[j] + ops[j][6] + Z["noise"](j), -j))
         if ops[k][0] != "x":
             free[ops[k][0]] = start[k] + ops[k][5]
         done = start[k] + ops[k][5] + late[ops[k][4]] + Z["wake"]
@@ -137,10 +143,83 @@ def arrange(ops, deps):
     return order
 
 
+def polish(ops, deps, order):
+    n = len(ops)
+    names = sorted({op[0] for op in ops})
+    eng = [names.index(op[0]) for op in ops]
+    far = names.index("x")
+    after = [set() for _ in ops]
+    for k, d in enumerate(deps):
+        for j in d:
+            after[j].add(k)
+    def listed(op):
+        return any(v[0] in ("cu", "wu") for v in op[2])
+
+    cost = [[op[5] * (u if op[4] == "arrive" else 1.0 if op[4] != "c" else s * (1.0 - (1.0 - x) * (1.0 - 65.0 / op[5])) if listed(op) else s)
+             for op in ops] for s, u, x, w in Z["speeds"]]
+    lates = [[(Z["load"] if op[4] == "dma" else 0.0) + w for op in ops] for s, u, x, w in Z["speeds"]]
+
+    def run(order, lo, old):
+        total, fins = 0.0, []
+        last = {eng[k]: k for k in order[:lo]}
+        for c, f, late in zip(cost, old, lates):
+            fin, free = list(f), [0.0] * len(names)
+            for e, k in last.items():
+                if e != far:
+                    free[e] = fin[k] - late[k]
+            for k in order[lo:]:
+                e = eng[k]
+                t = free[e]
+                for j in deps[k]:
+                    if fin[j] > t:
+                        t = fin[j]
+                t += c[k]
+                if e != far:
+                    free[e] = t
+                fin[k] = t + late[k]
+            total += max(fin) + Z["soon"] * sum(fin)
+            fins.append(fin)
+        return total / len(cost), fins
+
+    cur, fin = run(order, 0, [[0.0] * n for _ in cost])
+    best, s, tries = (cur, order), 1, Z["tries"]
+    for it in range(tries):
+        s = (s * 1103515245 + 12345) % 2147483648
+        i = (s >> 8) % n
+        k = order[i]
+        if ops[k][4] != "c":
+            continue
+        s = (s * 1103515245 + 12345) % 2147483648
+        step, hops = 1 if s >> 20 & 1 else -1, 1 + (s >> 12) % 3
+        j, block = i, after[k] if step > 0 else deps[k]
+        while hops and 0 <= j + step < n and order[j + step] not in block:
+            j += step
+            hops -= eng[order[j]] == eng[k]
+        if hops:
+            continue
+        new = order[:i] + order[i + 1:]
+        new.insert(j, k)
+        v, f2 = run(new, min(i, j), fin)
+        s = (s * 1103515245 + 12345) % 2147483648
+        if v <= cur - Z["slack"] * (1 - it / tries) * math.log((s + 1) / 2147483649.0):
+            cur, order, fin = v, new, f2
+            if v < best[0]:
+                best = (v, new)
+            if it % 16 == 0:
+                order = sorted(order, key=lambda k: fin[0][k] - lates[0][k] - cost[0][k])
+    return best[1]
+
+
+ORDER = {}
+
+
 def emit(g, T, ops):
     queue = {"v": g.vector, "a": g.scalar, "p": g.tensor, "s": g.sync, "g": g}
     deps = needs(ops)
-    order = arrange(ops, deps)
+    key = str([op[2:] for op in ops])
+    if key not in ORDER:
+        ORDER[key] = polish(ops, deps, arrange(ops, deps))
+    order = ORDER[key]
     place = {k: i for i, k in enumerate(order)}
     deps = [{place[j] for j in deps[k]} for k in order]
     ops = [ops[k] for k in order]
@@ -242,7 +321,7 @@ def rank_program(g, core, T, topo):
         return 0.83 * max(64.0, size(a) * rate)
 
     def put(eng, fn, rd, wr, t, kind="c", boost=0.0):
-        ops.append((eng, fn, rd, wr, kind, t, boost))
+        ops.append((eng, fn, rd, wr, kind, t + Z["each"][eng == "a"], boost))
 
     def copy(out, src, eng="v"):
         if eng == "a":
@@ -303,8 +382,8 @@ def rank_program(g, core, T, topo):
     def heads(out, src, n, w, c):
         put("g", lambda q: q.affine_select(ap(out), ap(src), [[0, n], [1, w]], A.is_gt, c, 0, 0), [src], [out], 170.0 + 1.66 * n * w)
 
-    def dma(eng, out, src, rd, wr):
-        put(eng, lambda q: q.dma_start(out, src), rd, wr, 50.0, "dma")
+    def dma(eng, out, src, rd, wr, t=50.0):
+        put(eng, lambda q: q.dma_start(out, src), rd, wr, t, "dma")
 
     def col(k):
         return V("col", k, k + 1)
@@ -312,16 +391,18 @@ def rank_program(g, core, T, topo):
     def ends(name, n, w, lo=0):
         return V(name, lo * w + w - 1, n * w, w)
 
-    def gather(out, win, lst, share):
-        n = PART[lst][2]
-        cut = 2 * int(n * share / 2 + 0.5)
-        for eng, a, b in (("v", 0, cut), ("a", cut, n)):
+    def gather(out, win, lst, share, lo, hi, shift=0):
+        cut = lo + 2 * int((hi - lo) * share / 2 + 0.5)
+        for eng, a, b in (("v", lo, cut), ("a", cut, hi)):
             if b > a:
-                copy(V(out, 16 * a, 16 * b), by(win, V(lst, a, b)), eng)
+                copy(V(out, shift + 16 * a, shift + 16 * b), by(win, V(lst, a, b)), eng)
 
-    cH, cE, cA, cJ, cA4, cT, cS4, cS16, cS1, c2A, cTH, cU, cU4, cN, cN2, cX, cY, cA1 = range(18)
+    cH, cE, cA, cJ, cA4, cT, cS4, cS16, cS1, c2A, cTH, cU, cU4, cN, cN2, cX, cY, cA1, cN3, cT8 = range(20)
+    WHOLE, PARTS = ((0, H),), ((0, 64), (64, H))
 
-    dma("s", ap(V("X", 0, 768)), T.x[:, :], [], [V("X", 0, 768)])
+    dma("s", ap(V("X0", 0, 384)), T.x[:, 0:384], [], [V("X0", 0, 384)])
+    dma("a", ap(V("X", 384, 768)), T.x[:, 384:768], [], [V("X", 384, 768)], 250.0)
+    dma("s", ap(V("X", 0, 384)), T.x[:, 0:384], [], [V("X", 0, 384)])
     dma("s", ap(V("qw")).bitcast(dt.uint8), T.wc[:, :], [], [V("qw")])
     dma("s", ap(V("sw")), T.ws[:, :], [], [V("sw")])
     dma("s", ap(V("vt")), T.v[:, :], [], [V("vt")])
@@ -333,9 +414,8 @@ def rank_program(g, core, T, topo):
     iota(V("k16"), [[0, 6], [1, 16]])
     iota(V("irep", 0, 6), [[32, 6]], 31)
     iota(V("irep", 6, 12), [[4, 6]], 3)
-    iota(V("irep", 12, 18), [[32, 3], [H, 2]], 31)
-    iota(V("irep", 18, 24), [[16, 6]], 15)
-    iota(V("n4"), [[64, 2]], 31)
+    iota(V("irep", 12, 16), [[32, 2], [64, 2]], 31)
+    iota(V("irep", 16, 18), [[32, 2]], 31)
     iota(V("k4"), [[0, 48], [1, 4]])
     iota(V("k32"), [[0, 2], [1, 32]])
     iota(V("k2"), [[1, 32], [0, 2]])
@@ -344,12 +424,12 @@ def rank_program(g, core, T, topo):
     heads(V("t32"), V("big"), 6, 32, TINY)
     heads(V("r32"), V("one"), 3, 32, 0.0)
     heads(V("r16"), V("one"), 6, 16, 0.0)
-    heads(V("r16b"), V("one"), 6, 16, 0.0)
     iota(V("vals"), [[1, C]])
     iota(V("ka4"), [[0, 6], [1, 4], [0, 4]])
     iota(V("base"), [[8, 24], [0, 4]])
     iota(V("r4"), [[0, 8], [64, 4]])
-    for v in (V("th", 24, 32), V("cz", 0, C, 2), V("zt"), V("SX", 768, 776), V("AR", 768, 776), V("Mt", 384, 512)):
+    for v in (V("th", 24, 32), V("cz", 0, C, 2), V("zt"), V("SX", 768, 776), V("AR", 512, 528),
+              V("AR", 784, 1040), V("Mt", 384, 512)):
         zero(v)
 
     def same(out, a, c):
@@ -372,25 +452,28 @@ def rank_program(g, core, T, topo):
     copy(V("col", 2, 6), V("ic", 2, 6))
     ts(V("iw"), V("iu"), 3 * 4096 + 15, A.bitwise_and)
     tt(V("rq"), V("iw"), V("rl"), A.add)
-    ts(V("op2"), V("rq"), float(C), A.min)
+    fill(V("X0", 384, 512), 0.0)
     ts(V("op1"), V("rq"), float(H), A.min)
+    ts(V("opf", 0, 16), V("rq", 0, 16), 64.0, A.min, 2.0, A.mult)
+    ts(V("opf", 16, 24), V("rq", 0, 8), 32.0, A.min, 2.0, A.mult)
     ts(V("op3"), V("rq"), float(H), A.min, 2.0, A.mult)
-    ts(V("opf"), V("rq"), float(H), A.min, 2.0, A.mult)
     ts(V("op4"), V("opf"), 1.0, A.add)
-    ts(col(cN2), col(cA4), 2.0, A.is_ge, 32.0 - C, A.mult)
-    act(col(cN), col(cA4), ACT.Identity, scale=float(H), bias=col(cN2))
-    ts(V("on4"), V("n4"), col(cN), A.add, float(C - 1), A.min)
+    ts(col(cN2), col(cA4), 2.0, A.is_ge, -96.0, A.mult)
+    act(col(cN), col(cA4), ACT.Identity, scale=64.0, bias=col(cN2))
+    ts(V("on4", 0, 1), col(cN), 31.0, A.add)
+    act(col(cN3), col(cA4), ACT.Identity, scale=32.0, bias=31.0)
+    ts(V("on4", 2, 3), col(cN3), 63.0, A.min)
     ts(col(cS1), col(cA4), 3.0, A.is_equal, 1.0 / RADIX, A.max)
     ts(col(cS16), col(cA), 15.0, A.is_equal, 1.0 / RADIX, A.max)
     act(col(cU), col(cA), ACT.Identity, scale=-1.0, bias=-1.0)
     act(col(cU4), col(cA4), ACT.Identity, scale=-1.0, bias=-1.0)
     act(col(cA1), col(cA), ACT.Identity, bias=-0.5)
-    same(V("d16"), V("k16"), col(cA))
-    same(V("eye"), V("k32"), col(cJ))
+    ts(V("d16"), V("k16"), col(cA), A.is_equal)
+    ts(V("eye"), V("k32"), col(cJ), A.is_equal)
     same(V("eye2"), V("k2"), col(cJ))
     radix(V("g16"), V("k16"), V("s16"), col(cU))
     radix(V("g4"), V("k4"), V("k4"), col(cU4))
-    copy(V("orep"), V("irep"))
+    copy(V("orep", 0, 18), V("irep", 0, 18))
     act(V("mul"), V("k16"), ACT.Sign, scale=-1.0, bias=col(cA1))
     act(V("mul"), V("mul"), ACT.Relu, scale=1.0 - BELOW)
     act(V("mul"), V("mul"), ACT.Identity, scale=-1.0, bias=1.0)
@@ -401,7 +484,6 @@ def rank_program(g, core, T, topo):
     act(V("base"), V("base"), ACT.Identity, bias=col(c2A))
     act(V("b2"), ends("base", 24, 4), ACT.Identity, scale=2.0, bias=1.0)
 
-    REP, CREP, REP2, REP16 = (V("orep", k, k + 6) for k in (0, 6, 12, 18))
     PK, PG = ["pk0", "pk1", "pk2"], ["pg0", "pg1", "pg2"]
 
     def mask(out, src, h, eng):
@@ -410,112 +492,143 @@ def rank_program(g, core, T, topo):
         else:
             ts(out, src, V("colb", 1 - h, 2 - h), A.mult)
 
-    def products(k, kind, qf, sf, lst, banks, eye):
-        quant(V("qg" + kind), V("sg" + kind), V("G" + kind), Z["boost"])
-        for b, e in ((0, 2), (2, 3)):
-            copy(V("qs%d" % k, 128 * b, 128 * e), by(qf, V(lst, 8 * b, 8 * e)))
-            act(V("ss%d" % k, 128 * b, 128 * e), by(sf, V(lst, 8 * b, 8 * e)))
-        for b in range(3):
-            lo = min(64 * b, 64)
+    def products(k, kind, a, e, qf, sf, lst, banks, eye):
+        n = max(128, 2 * (e - a))
+        lo, at = 2 * e - n, 2 * a
+        quant(V("qg" + kind, at, at + n), V("sg" + kind, at, at + n), V("G" + kind, 4 * lo, 4 * (lo + n)), Z["boost"])
+        for x, y in PARTS:
+            if a <= x and y <= e:
+                copy(V("qs%d" % k, 4 * x, 4 * y), by(qf, V(lst, x // 4, y // 4)))
+                act(V("ss%d" % k, 4 * x, 4 * y), by(sf, V(lst, x // 4, y // 4)))
+        for b in range(a // 32, e // 32):
+            c = 64 * b - lo
+            w = min(c, n - 128)
             mm(V(banks[b], 0, 128), V("qs%d" % k, 128 * b, 128 * b + 128), V("ss%d" % k, 128 * b, 128 * b + 128),
-               V("qg" + kind, lo, lo + 128), V("sg" + kind, lo, lo + 128))
-            tt(V("D" + kind, 64 * b, 64 * b + 64), V(banks[b], 64 * b - lo, 64 * b - lo + 64), V(eye), A.mult)
+               V("qg" + kind, at + w, at + w + 128), V("sg" + kind, at + w, at + w + 128))
+            tt(V("D" + kind, 64 * b, 64 * b + 64), V(banks[b], c - w, c - w + 64), V(eye), A.mult)
 
-    def sizes(k, kind, lo, qf, sf, lst, banks, nact):
-        for n, (b, h) in enumerate([(b, h) for b in range(3) for h in range(2)]):
-            mask(V("G" + kind, 256 * b + 128 * h, 256 * b + 128 * h + 128), V("X", lo + 128 * b, lo + 128 * b + 128), h, "a" if n < nact else "v")
-        products(k, kind, qf, sf, lst, banks, "eye")
-        for a, e in ((0, 128), (128, C)):
-            scan(V("E" + kind, a, e), V("t32", a, e), V("D" + kind, a, e), 1.0, A.min, A.add)
-        tt(V("prw" + kind), by(V("E" + kind), REP), V("d16"), A.mult)
-        copy(V("pre" + kind), by(V("E" + kind), REP), Z["pre"])
+    def sizes(k, kind, a, e, name, lo, qf, sf, lst, banks, share):
+        todo = [(b, h) for b in range(a // 32, e // 32) for h in range(2)]
+        for n, (b, h) in enumerate(todo):
+            mask(V("G" + kind, 256 * b + 128 * h, 256 * b + 128 * h + 128), V(name, lo + 128 * b, lo + 128 * b + 128), h,
+                 "a" if n < share * len(todo) else "v")
+        products(k, kind, a, e, qf, sf, lst, banks, "eye")
+        for x, y in PARTS:
+            if a <= x and y <= e:
+                w = 64 if k > 1 else 2 * (y - x)
+                for c in range(2 * x, 2 * y, w):
+                    scan(V("E" + kind, c, c + w), V("t32", c, c + w), V("D" + kind, c, c + w), 1.0, A.min, A.add)
+                src = by(V("E" + kind, 2 * x, 2 * y), V("orep", 0, (y - x) // 16))
+                tt(V("prw" + kind, x, y), src, V("d16", x, y), A.mult)
+                copy(V("pre" + kind, x, y), src, "a")
+
+    def place(a):
+        return 8 * a + (16 if a >= 64 else 0)
 
     def paired(k, kind, name, lst, banks, nact):
-        qf, sf = V("qf%d" % k), V("sf%d" % k)
-        quant(qf, sf, V(name))
-        for n, (e, h) in enumerate([(e, h) for e in range(4) for h in range(2)]):
-            mask(V("G" + kind, 4 * h + e, 768, 8), V(name, 4 + e, 768, 8), h, "a" if n < nact else "v")
-        products(k, kind, qf, sf, lst, banks, "eye2")
-        for a, e in ((0, 64), (64, H)):
+        gap = 4 if kind == "R" else 0
+        if gap:
+            wins = [(V("qf%d" % k, 0, 130), V("sf%d" % k, 0, 130)), (V("qf%d" % k, 160, 288), V("sf%d" % k, 160, 288))]
+            quant(*wins[0], V(name, 0, 520))
+            quant(*wins[1], V(name, 528, 1040))
+        else:
+            wins = [(V("qf%d" % k, 0, C + 2), V("sf%d" % k, 0, C + 2))] * 2
+            quant(*wins[0], V(name))
+        hi = 4 * (C + gap)
+        for n, (u, h) in enumerate([(u, h) for u in range(4) for h in range(2)]):
+            mask(V("G" + kind, 4 * h + u, hi, 8), V(name, 4 + u, hi, 8), h, "a" if n < nact else "v")
+        quant(V("qg" + kind, 0, C + gap), V("sg" + kind, 0, C + gap), V("G" + kind, 0, hi), Z["boost"])
+        for (x, y), (qf, sf) in zip(PARTS, wins):
+            copy(V("qs%d" % k, 4 * x, 4 * y), by(qf, V(lst, x // 4, y // 4)))
+            act(V("ss%d" % k, 4 * x, 4 * y), by(sf, V(lst, x // 4, y // 4)))
+        for b, w, c in ((0, 0, 0), (1, 0, 64), (2, 64 + gap, 64)):
+            mm(V(banks[b], 0, 128), V("qs%d" % k, 128 * b, 128 * b + 128), V("ss%d" % k, 128 * b, 128 * b + 128),
+               V("qg" + kind, w, w + 128), V("sg" + kind, w, w + 128))
+            tt(V("D" + kind, 64 * b, 64 * b + 64), V(banks[b], c, c + 64), V("eye2"), A.mult)
+        for a, e in PARTS:
             for h in range(2):
-                out, d = V("E" + kind, H * h + a, H * h + e), V("D" + kind, 2 * a + h, 2 * e, 2)
+                lo = 2 * a + h * (e - a)
+                out, d = V("E" + kind, lo, lo + e - a), V("D" + kind, 2 * a + h, 2 * e, 2)
                 if kind == "A":
                     scan(out, V("r32", a, e), d, 0.0, A.mult, A.add)
                 else:
                     scan(out, V("t32", a, e), d, 1.0, A.min, A.add)
 
-    def spread(kind, lo):
-        turn(V("own" + kind), V("prw" + kind))
-        turn(V("row", lo, lo + H), V("pre" + kind))
-        scan(V("ow" + kind), V("r16"), V("own" + kind), 0.0, A.mult, A.add)
-        tt(V("mix" + kind), V("row", lo, lo + H), V("mul"), A.mult)
-        tt(V("fm" + kind), by(V("ow" + kind), REP16), V("mix" + kind), A.is_gt)
-        scan(V("in" + kind), V("r16b"), V("fm" + kind), 0.0, A.mult, A.add)
+    def spread(kind, row, lo):
+        for a, e in (PARTS if Z["pk"] > 1 and kind == "K" else WHOLE):
+            turn(V("own" + kind, a, e), V("prw" + kind, a, e))
+            turn(V(row, lo + a, lo + e), V("pre" + kind, a, e))
+            scan(V("ow" + kind, a, e), V("r16", a, e), V("own" + kind, a, e), 0.0, A.mult, A.add)
+            tt(V("mix" + kind, a, e), V(row, lo + a, lo + e), V("mul", a, e), A.mult)
 
-    def count(on_act, w, o, signs, flags, res, more):
-        n = size(w)
+    def count(on_act, ws, o, signs, flags, res, more=None):
         name, at = res
+        buf, lo = signs if on_act else flags
+        n = 0
+        for w in ws:
+            out = V(buf, lo + n, lo + n + size(w))
+            n += size(w)
+            if on_act:
+                act(out, w, ACT.Sign, scale=-1.0, bias=o)
+            else:
+                ts(out, w, o, A.is_lt)
         if on_act:
-            act(V(signs[0], signs[1], signs[1] + n), w, ACT.Sign, scale=-1.0, bias=o)
-            s = V(signs[0], signs[1], signs[1] + n + 1)
+            s = V(buf, lo, lo + n + (1 if more else 0))
             act(s, s, ACT.Relu, acc=V(name, at, at + 1))
         else:
-            ts(V(flags[0], flags[1], flags[1] + n), w, o, A.is_lt)
-            scan(V(name, at + 1 - n // 2, at + 1), V(flags[0], flags[1], flags[1] + n // 2), V(flags[0], flags[1] + n // 2, flags[1] + n),
-                 more, A.add, A.add)
+            scan(V(name, at + 1 - n // 2, at + 1), V(buf, lo, lo + n // 2), V(buf, lo + n // 2, lo + n), more or 0.0, A.add, A.add)
 
     def end16(name, m):
         return V(name, 16 * m + 15, 16 * m + 16)
 
-    def old_half(nact):
-        spread("S", 0)
-        act(V("cs", 0, WS), V("row", 16, H))
-        act(V("cs", WS, 2 * WS), V("row", 0, WS), scale=BELOW)
-        act(V("row", C, C + H), V("row", 0, H), scale=BELOW)
-        if nact:
-            act(ends("snS", nact, WS + 1), ends("inS", nact, 16))
-        for m in range(CH):
-            count(m < nact, V("cs", 16 * m, 16 * m + WS), end16("owS", m), ("snS", (WS + 1) * m), ("fs", WS * m),
-                  ("sn", (H + 1) * m + H), end16("inS", m))
+    def old_half(row):
+        spread("S", row, 0)
+        act(V("row", C, C + H), V(row, 0, H), scale=BELOW)
+        if row == "rs":
+            act(V("rs", H, H + WS), V("rs", 0, WS), scale=BELOW)
+            act(V("row", 0, H), V("rs", 0, H))
+            for m in range(CH):
+                count(m < Z["ss"], [V("rs", 16 + 16 * m, 16 + 16 * m + WS), V("mixS", 16 * m, 16 * m + 16)], end16("owS", m),
+                      ("snS", H * m), ("fs", H * m), ("sn", (H + 1) * m + H))
 
-    def new_half(nsk, nkk):
-        spread("K", H)
+    def new_half(t):
+        spread("K", "row", H)
         act(V("row", C + H, C + H + WS), V("row", H, H + WS), scale=BELOW)
+        nkk = Z["kk" if t else "kk0"]
+        first = len(ops)
         for m in range(CH):
-            at = (H + 1) * m
-            count(m < nsk, V("row", H, C), end16("owS", m), ("sn", at), ("fx", H * m), ("fin", SLOT * m + SLOT - 1), V("sn", at + H, at + H + 1))
-        if nkk:
-            act(ends("snK", nkk, WK + 1), ends("inK", nkk, 16))
+            at, res = (H + 1) * m, ("fin", SLOT * m + SLOT - 1)
+            if t == 0:
+                count(m < Z["sk0"], [V("row", 16 + 16 * m, 16 + 16 * m + WK), V("mixS", 16 * m, 16 * m + 16)], end16("owS", m),
+                      ("snW", C * m), ("fw", C * m), res)
+            else:
+                count(m < Z["sk"], [V("row", H, C)], end16("owS", m), ("sn", at), ("fx", H * m), res, V("sn", at + H, at + H + 1))
+        copy(V("ork", 0, CH), ends("fin", CH, SLOT))
+        ops[first:] = [op[:6] + (Z["early"],) for op in ops[first:]]
+        copy(by(V("O"), V("ork", 0, CH)), V("vals", 0, H))
+        ops[-1] = ops[-1][:6] + (Z["late"],)
         for m in range(CH):
             res = ("fin", SLOT * (CH + m) + SLOT - 1) if m < nkk else ("cn", SLOT * m + SLOT - 1)
             lo = H + 16 + 16 * m
-            count(m < nkk, V("row", lo, lo + WK), end16("owK", m), ("snK", (WK + 1) * m), ("fk", WK * m), res, end16("inK", m))
-        if Z["split"]:
-            copy(V("ork", 0, CH), ends("fin", CH, SLOT))
-            copy(by(V("O"), V("ork", 0, CH)), V("vals", 0, H))
-            if nkk:
-                copy(V("ork", CH, CH + nkk), ends("fin", CH + nkk, SLOT, CH))
-        else:
-            copy(V("ork", 0, CH + nkk), ends("fin", CH + nkk, SLOT))
+            count(m < nkk, [V("row", lo, lo + WK), V("mixK", 16 * m, 16 * m + 16)], end16("owK", m), ("snK", C * m), ("fk", C * m), res)
+        copy(V("ork", CH, CH + nkk), ends("fin", CH + nkk, SLOT, CH))
         copy(V("ork", CH + nkk, 12), ends("cn", CH, SLOT, nkk))
-        if Z["split"]:
-            copy(by(V("O"), V("ork", CH, 12)), V("vals", H, C))
-        else:
-            copy(by(V("O"), V("ork")), V("vals"))
+        copy(by(V("O"), V("ork", CH, 12)), V("vals", H, C))
 
-    quant(V("qf0"), V("sf0"), V("X"))
-    sizes(0, "S", 0, V("qf0"), V("sf0"), "op2", PK, Z["mk0"] // 2)
-    sizes(1, "K", 384, V("qf0", 96, 224), V("sf0", 96, 224), "op1", PG, Z["mk0"] - Z["mk0"] // 2)
-    old_half(Z["ss0"])
+    quant(V("qf0", 0, 128), V("sf0", 0, 128), V("X0"))
+    sizes(0, "S", 0, H, "X0", 0, V("qf0", 0, 128), V("sf0", 0, 128), "op1", PK, Z["mk0"][0])
+    quant(V("qf0", 128, 256), V("sf0", 128, 256), V("X", 384, 896))
+    sizes(1, "K", 0, H, "X", 384, V("qf0", 128, 256), V("sf0", 128, 256), "op1", PG, Z["mk0"][1])
+    old_half("row")
 
     for t in range(R):
         stage = 2 + 3 * t
-        new_half(Z["sk" if t else "sk0"], Z["kk" if t else "kk0"])
+        new_half(t)
         scan(V("lx"), V("g4"), V("O"), 0.0, A.mult, A.add)
         scan(V("ld"), V("g16"), V("O", 0, C, 2), 0.0, A.mult, A.add)
         ts(V("ox"), ends("lx", 48, 4), col(cS4), A.mult, col(cT), A.add)
         ts(V("od"), ends("ld", CH, 16), col(cS16), A.mult)
-        gather("SX", V("X", 0, 768), "ox", Z["gx"])
+        gather("SX", V("X", 0, 768), "ox", 0.5, 0, 48)
         if t == R - 1:
             act(V("Of"), V("O"))
             dma("s", T.ol[:, :], T.Of[0:128:16, :], [V("Of")], [])
@@ -527,51 +640,65 @@ def rank_program(g, core, T, topo):
         act(V("th", 3, 24, 4), V("th", 0, 24, 4), scale=-BELOW)
         act(V("th", 2, 24, 4), V("th", 1, 24, 4), scale=-BELOW)
         tt(V("dam"), V("dap"), V("ka4"), A.max)
-        paired(stage, "A", "SX", "op3", PK, Z["ma"])
-
-        tt(V("cp"), by(V("EA"), V("on4")), V("th"), A.is_ge)
-        scan(V("cq"), V("r4"), V("cp"), 0.0, A.min, A.add)
-        ts(V("ncp"), by(V("cq"), CREP), -0.5, A.mult, 1.0, A.add)
-        turn(V("cz", 1, C, 2), V("ncp"))
-        for e in range(4):
-            scan(V("AR", e, 768, 4), V("cz"), V("SX", e, 768, 4), 0.0, A.mult, A.add)
-
-        paired(stage + 1, "R", "AR", "op4", PG, Z["mr"])
-        tt(V("swp"), by(V("ER"), REP2), V("dam"), A.is_ge)
-        turn(V("swr"), V("swp"))
-        scan(V("lm"), V("base"), V("swr"), 0.0, A.max, A.add)
-        ts(V("om"), ends("lm", 24, 4), 4.0, A.mult, col(cT), A.add)
-        gather("Mt", V("AR", 0, 768), "om", Z["gm"])
-        qm, sm = "qm%d" % t, "sm%d" % t
-        quant(V(qm), V(sm), V("Mt"))
         dst = T.cores[(rank + STEP[t]) % N]
         src = T.cores[(rank - STEP[t]) % N]
         rid, pid = topo.addr(dst, core)
-        engines = topo.mask(core, dst)
-        neng = len(topo.engines(core, dst))
         at = 128 + H * t
-        arr = T.sem["arr%d" % t]
+        qm, sm = "qm%d" % t, "sm%d" % t
 
-        def send(out, src, arr=arr, rid=rid, pid=pid, engines=engines, neng=neng):
+        def share(a, b, k, t=t):
+            return topo.engines(a, b)[k::2] if t == 0 else topo.engines(a, b)
+
+        def send(out, src, arr, engines, rid=rid, pid=pid):
             def go(q):
-                q.remote_dma(out, src, arr, T.sem.sent, pid, rid, engines)
-                return neng
+                q.remote_dma(out, src, arr, T.sem.sent, pid, rid, sum(1 << e for e in engines))
+                return len(engines)
             return go
 
-        lq, ls = V("ql", at, at + H), V("sl", at, at + H)
-        put("g", send(ap(lq).bitcast(dt.uint8), ap(V(qm, 0, H)).bitcast(dt.uint8)), [V(qm, 0, H)], [], 100.0, "remote")
-        put("g", send(ap(ls), ap(V(sm, 0, H))), [V(sm, 0, H)], [], 100.0, "remote")
-        put("x", (arr, 2 * len(topo.engines(src, core))), [V(qm, 0, H)], [lq, ls], Z["send"], "arrive")
+        paired(stage, "A", "SX", "op3", PK, Z["ma"])
 
-        tt(V("ls"), V("b2"), ends("lm", 24, 4), A.subtract)
-        ts(V("oz"), V("ls"), 4.0, A.mult, col(cT), A.add)
-        gather("X", V("AR", 0, 768), "oz", 0.0)
+        for s, (a, e) in enumerate(PARTS):
+            cp, cq = V("cp", 16 * s, 16 * s + 16), V("cq", 16 * s, 16 * s + 16)
+            tt(cp, by(V("EA", 2 * a, 2 * e), V("on4", 2 * s, 2 * s + 1)), V("th", 16 * s, 16 * s + 16), A.is_ge)
+            scan(cq, V("r4", 0, 16), cp, 0.0, A.min, A.add)
+            ts(V("ncp", a, e), by(cq, V("orep", 6, 6 + (e - a) // 16)), -0.5, A.mult, 1.0, A.add)
+            turn(V("cz", 2 * a + 1, 2 * e, 2), V("ncp", a, e))
+            lo = place(a)
+            hi = lo + 8 * (e - a)
+            for u in range(4):
+                scan(V("AR", lo + u, hi, 4), V("cz", 2 * a, 2 * e), V("SX", 8 * a + u, 8 * e, 4), 0.0, A.mult, A.add)
+
+        paired(stage + 1, "R", "AR", "op4", PG, Z["mr"])
+        for s, (a, e) in enumerate(PARTS):
+            lo = place(a)
+            hi = lo + 8 * (e - a)
+            rep = V("orep", 12 + a // 16, 12 + e // 16)
+            tt(V("swp", a, e), by(V("ER", 2 * a, 2 * e), rep), V("dam", a, e), A.is_ge)
+            turn(V("swr", a, e), V("swp", a, e))
+            scan(V("lm", a, e), V("base", 0, e - a), V("swr", a, e), 0.0, A.max, A.add)
+            ts(V("om", a // 4, e // 4), ends("lm", e // 4, 4, a // 4), 4.0, A.mult, col(cT), A.add)
+            gather("Mt", V("AR", lo, hi), "om", Z["gm"][s], a // 4, e // 4)
+            if Z["sends"][t] == 2 or s:
+                x = a if Z["sends"][t] == 2 else 0
+                quant(V(qm, 2 * x, 2 * x + 128), V(sm, 2 * x, 2 * x + 128), V("Mt", 4 * x, 4 * x + 512))
+                arr = T.sem["arr%d" % (2 * t + s)]
+                lq, ls = V("ql", at + x, at + e), V("sl", at + x, at + e)
+                mq, ms = V(qm, 2 * x, x + e), V(sm, 2 * x, x + e)
+                put("g", send(ap(lq).bitcast(dt.uint8), ap(mq).bitcast(dt.uint8), arr, share(core, dst, 0)), [mq], [], 100.0, "remote")
+                put("g", send(ap(ls), ap(ms), arr, share(core, dst, 1)), [ms], [], 100.0, "remote")
+                put("x", (arr, len(share(src, core, 0) + share(src, core, 1))), [mq], [lq, ls], Z["send"], "arrive")
+
+            tt(V("ls", a // 4, e // 4), V("b2", 0, (e - a) // 4), ends("lm", e // 4, 4, a // 4), A.subtract)
+            ts(V("oz", a // 4, e // 4), V("ls", a // 4, e // 4), 4.0, A.mult, col(cT), A.add)
+            gather("X", V("AR", lo, hi), "oz", 0.0, a // 4, e // 4)
+            if t < R - 1:
+                tt(V("preS", a, e), by(V("ER", 2 * a, 2 * e), rep), V("dap", a, e), A.min)
+
         if t == 0:
             quant(V("ql", 0, 128), V("sl", 0, 128), V("zt"))
         if t < R - 1:
-            tt(V("preS"), by(V("ER"), REP2), V("dap"), A.min)
             tt(V("prwS"), V("preS"), V("d16"), A.mult)
-            old_half(Z["ss"])
+            old_half("rs")
         else:
             quant(V("qv"), V("sv"), V("vt"))
             quant(V("qxs"), V("sxs"), V("X", 0, 512))
@@ -582,16 +709,17 @@ def rank_program(g, core, T, topo):
             copy(V("yt", 0, H), V("py", 0, H))
             dma("s", T.y[:, 0:H], ap(V("yt", 0, H)), [V("yt", 0, H)], [])
 
-        for b in (2, 0, 3, 1):
-            mm(V("pk%d" % b, 0, 128), V("qw", 128 * b, 128 * b + 128), V("sw", 128 * b, 128 * b + 128),
-               V("ql", at - 32, at + H), V("sl", at - 32, at + H))
-        for b in (0, 1):
-            ts(V("X", 384 + b, 768, 4), V("pk%d" % b, 32, 128), 0.03125, A.mult)
-            act(V("X", 386 + b, 768, 4), V("pk%d" % (b + 2), 32, 128), scale=0.03125)
-        if t < R - 1:
-            qf, sf = V("qf%d" % (stage + 2), 0, 128), V("sf%d" % (stage + 2), 0, 128)
-            quant(qf, sf, V("X", 384, 896))
-            sizes(stage + 2, "K", 384, qf, sf, "op1", PG, Z["mk"])
+        for a, e in (PARTS if Z["sends"][t] == 2 else WHOLE):
+            for b in (2, 0, 3, 1):
+                mm(V("pk%d" % b, 0, 128), V("qw", 128 * b, 128 * b + 128), V("sw", 128 * b, 128 * b + 128),
+                   V("ql", at + e - 128, at + e), V("sl", at + e - 128, at + e))
+            for b in (0, 1):
+                ts(V("X", 384 + 4 * a + b, 384 + 4 * e, 4), V("pk%d" % b, 128 - e + a, 128), 0.03125, A.mult)
+                act(V("X", 386 + 4 * a + b, 384 + 4 * e, 4), V("pk%d" % (b + 2), 128 - e + a, 128), scale=0.03125)
+            if t < R - 1:
+                qf, sf = V("qf%d" % (stage + 2), 2 * a, 2 * a + 128), V("sf%d" % (stage + 2), 2 * a, 2 * a + 128)
+                quant(qf, sf, V("X", 384, 896))
+                sizes(stage + 2, "K", a, e, "X", 384, qf, sf, "op1", PG, Z["mk"])
 
     quant(V("qxk"), V("sxk"), V("X", 384, 896))
     mm(V("pg0", 0, 128), V("qv"), V("sv"), V("qxk"), V("sxk"))

import math

from concourse.mybir import dt, AluOpType, ActivationFunctionType

C, H, R = 192, 96, 3
STEP = [1, 2, 4]
TINY = 2.0 ** -100
BELOW = 1.0 - 2.0 ** -24
RADIX = 2.0 ** 20
HUGE = 2.0 ** 90
CH = 6
WS = H - 16
WK = WS + H
SLOT = 100
Z = dict(each=(8.0, 16.0), tries=70000, slack=7.0, speeds=((1.0, 1.0, 1.0, 220.0), (1.3, 0.7, 1.1, 220.0), (1.0, 0.9, 0.67, 250.0)), soon=0.002, late=-400.0, early=300.0, ss=3, sk=4, kk=2, gz=0.0, sc=6, sk0=3, kk0=2, mk=0.5, ma=5, mr=5, split=1, pre="aa", wake=215.0, send=1800.0, load=1400.0, fan=1.0, noise=lambda j: 0.0,
         mk0=(0.34, 0.67), gx=(0.5, 0.5), gm=(0.5, 0.5), boost=100.0, pk=2, sends=(1, 1, 1), qs=dict(A=0, R=1))

F, B, I, U = "float32", "bfloat16", "int32", "uint16"
X4, U8 = "float8_e4m3fn_x4", "uint8"


def _sb(n, d):
    return ("sbuf", [128, n], d)


SCRATCH = {
    "X": _sb(896, B), "SX": _sb(776, B), "AR": _sb(1040, B), "Mt": _sb(768, B), "vt": _sb(512, B), "zt": _sb(512, B),
    "qw": _sb(512, X4), "sw": _sb(512, U8), "qv": _sb(128, X4), "sv": _sb(128, U8),
    "ql": _sb(416, X4), "sl": _sb(416, U8),
    "qxs": _sb(128, X4), "sxs": _sb(128, U8), "qxk": _sb(128, X4), "sxk": _sb(128, U8),
    "yt": _sb(192, F), "Of": _sb(192, F), "ip": _sb(2, I), "ic": _sb(8, I), "iu": _sb(24, I), "iw": _sb(24, I), "irep": _sb(24, I),
}
for _k in "SKAR":
    SCRATCH["G" + _k], SCRATCH["qg" + _k], SCRATCH["sg" + _k] = _sb(768 if _k in "SK" else 784, B), _sb(256, X4), _sb(256, U8)
for _k in ("pk0", "pk1", "pk2", "pk3", "pg0", "pg1", "pg2", "py"):
    SCRATCH[_k] = ("psum", [128, 512], F)
SCRATCH["qf0"], SCRATCH["sf0"], SCRATCH["X0"] = _sb(256, X4), _sb(256, U8), _sb(512, B)
for _k in range(2, 10):
    SCRATCH["qf%d" % _k], SCRATCH["sf%d" % _k] = _sb(288, X4), _sb(288, U8)
for _k in range(10):
    SCRATCH["qs%d" % _k], SCRATCH["ss%d" % _k] = _sb(384, X4), _sb(384, U8)
for _k in range(R):
    SCRATCH["qm%d" % _k], SCRATCH["sm%d" % _k] = _sb(256, X4), _sb(256, U8)

PART = {}
for _buf, _dt, _names in (
        ("cf", F, (("col", 32), ("k32", 64), ("eye", 64), ("k2", 64), ("eye2", 64), ("one", 96), ("big", 192), ("r32", 96), ("t32", 192),
                   ("rl", 24), ("rq", 24), ("opf", 24), ("n6", 6), ("t16", 192), ("k16", 96), ("s16", 96), ("d16", 96), ("r16", 96), ("k4", 192),
                   ("mul", 96), ("ka4", 96), ("b2", 24))),
        ("cb", B, (("colb", 2), ("r4", 32), ("g16", 96), ("g4", 192), ("base", 96), ("vals", 192))),
        ("cu", U, (("op1", 24), ("op2", 24), ("op3", 24), ("op4", 24), ("orep", 24), ("on4", 4))),
        ("wf", F, (("DS", 192), ("DK", 192), ("DA", 192), ("DR", 192), ("ES", 192), ("EK", 192), ("EA", 192), ("ER", 192),
                   ("preS", 96), ("preK", 96), ("prwS", 96), ("prwK", 96), ("row", C + H + WS), ("ownS", 192), ("ownK", 192),
                   ("owS", 192), ("owK", 192), ("mixS", 96), ("mixK", 96), ("rs", H + WS), ("sn", CH * (H + 1)),
                   ("snS", CH * H), ("snK", CH * C), ("snW", CH * C), ("fin", 12 * SLOT),
                   ("da", 96), ("dap", 96), ("dam", 96), ("th", 32), ("cq", 32), ("ls", 24))),
        ("wb", B, (("fs", CH * H), ("fx", CH * H), ("fk", CH * C), ("fw", CH * C), ("cn", CH * SLOT), ("O", 192), ("lx", 192), ("ld", 96), ("cp", 32),
                   ("ncp", 96), ("cz", 192), ("swp", 96), ("swr", 96), ("lm", 96))),
        ("wu", U, (("ork", 12), ("ox", 48), ("od", 6), ("om", 24), ("oz", 24)))):
    _at = 0
    for _n, _w in _names:
        PART[_n] = (_buf, _at, _w)
        _at += (_w + 15) // 16 * 16
    SCRATCH[_buf] = _sb(_at, _dt)

NPOOL = 123
SEMAPHORES = ["c%d" % k for k in range(NPOOL)] + ["d%d" % k for k in range(20)] + ["arr%d" % k for k in range(2 * R)] + ["sent"]


def V(name, lo=0, hi=None, step=1):
    if name in PART:
        buf, at, w = PART[name]
        return (buf, at + lo, at + (w if hi is None else hi), step)
    return (name, lo, SCRATCH[name][1][1] if hi is None else hi, step)


def _bits(v):
    if SCRATCH[v[0]][0] == "psum":
        return 1
    if v[3] == 1:
        return ((1 << (v[2] - v[1])) - 1) << v[1]
    m = 0
    for i in range(v[1], v[2], v[3]):
        m |= 1 << i
    return m


def needs(ops):
    hist, out = {}, []
    for k, op in enumerate(ops):
        rd, wr = op[2], op[3]
        deps = set()
        acc = [(v, SCRATCH[v[0]][0] == "psum") for v in rd] + [(v, True) for v in wr]
        for v, w in acc:
            m = _bits(v)
            for j, mj, wj in hist.get(v[0], []):
                if (w or wj) and m & mj:
                    deps.add(j)
        for v, w in acc:
            m = _bits(v)
            old = hist.get(v[0], [])
            if w:
                old = [(j, mj & ~m, wj) for j, mj, wj in old if mj & ~m]
            hist[v[0]] = old + [(k, m, w)]
        deps.discard(k)
        out.append(deps)
    return out


def arrange(ops, deps):
    n = len(ops)
    late = {"dma": Z["load"], "remote": 0.0, "arrive": 0.0, "c": 0.0}
    after = [[] for _ in ops]
    for k, d in enumerate(deps):
        for j in d:
            after[j].append(k)
    chain = [0.0] * n
    for k in range(n - 1, -1, -1):
        ahead, most = {}, 0.0
        for j in sorted(after[k], key=lambda j: ops[j][5] - chain[j]):
            most = max(most, Z["wake"] + Z["fan"] * ahead.get(ops[j][0], 0.0) + chain[j])
            ahead[ops[j][0]] = ahead.get(ops[j][0], 0.0) + ops[j][5]
        chain[k] = ops[k][5] + late[ops[k][4]] + most
    left = [len(d) for d in deps]
    due = [0.0] * n
    ready = {k for k in range(n) if not left[k]}
    free, order = {}, []
    while ready:
        start = {k: max(due[k], free.get(ops[k][0], 0.0)) for k in ready}
        first = min(ready, key=lambda k: (start[k] + ops[k][5], k))
        end = start[first] + ops[first][5]
        k = max((j for j in ready if ops[j][0] == ops[first][0] and start[j] < end), key=lambda j: (chain[j] + ops[j][6] + Z["noise"](j), -j))
        if ops[k][0] != "x":
            free[ops[k][0]] = start[k] + ops[k][5]
        done = start[k] + ops[k][5] + late[ops[k][4]] + Z["wake"]
        ready.discard(k)
        order.append(k)
        for j in after[k]:
            left[j] -= 1
            due[j] = max(due[j], done)
            if not left[j]:
                ready.add(j)
    return order


def polish(ops, deps, order):
    n = len(ops)
    names = sorted({op[0] for op in ops})
    eng = [names.index(op[0]) for op in ops]
    far = names.index("x")
    after = [set() for _ in ops]
    for k, d in enumerate(deps):
        for j in d:
            after[j].add(k)
    def listed(op):
        return any(v[0] in ("cu", "wu") for v in op[2])

    cost = [[op[5] * (u if op[4] == "arrive" else 1.0 if op[4] != "c" else s * (1.0 - (1.0 - x) * (1.0 - 65.0 / op[5])) if listed(op) else s)
             for op in ops] for s, u, x, w in Z["speeds"]]
    lates = [[(Z["load"] if op[4] == "dma" else 0.0) + w for op in ops] for s, u, x, w in Z["speeds"]]

    def run(order, lo, old):
        total, fins = 0.0, []
        last = {eng[k]: k for k in order[:lo]}
        for c, f, late in zip(cost, old, lates):
            fin, free = list(f), [0.0] * len(names)
            for e, k in last.items():
                if e != far:
                    free[e] = fin[k] - late[k]
            for k in order[lo:]:
                e = eng[k]
                t = free[e]
                for j in deps[k]:
                    if fin[j] > t:
                        t = fin[j]
                t += c[k]
                if e != far:
                    free[e] = t
                fin[k] = t + late[k]
            total += max(fin) + Z["soon"] * sum(fin)
            fins.append(fin)
        return total / len(cost), fins

    cur, fin = run(order, 0, [[0.0] * n for _ in cost])
    best, s, tries = (cur, order), 1, Z["tries"]
    for it in range(tries):
        s = (s * 1103515245 + 12345) % 2147483648
        i = (s >> 8) % n
        k = order[i]
        if ops[k][4] != "c":
            continue
        s = (s * 1103515245 + 12345) % 2147483648
        step, hops = 1 if s >> 20 & 1 else -1, 1 + (s >> 12) % 3
        j, block = i, after[k] if step > 0 else deps[k]
        while hops and 0 <= j + step < n and order[j + step] not in block:
            j += step
            hops -= eng[order[j]] == eng[k]
        if hops:
            continue
        new = order[:i] + order[i + 1:]
        new.insert(j, k)
        v, f2 = run(new, min(i, j), fin)
        s = (s * 1103515245 + 12345) % 2147483648
        if v <= cur - Z["slack"] * (1 - it / tries) * math.log((s + 1) / 2147483649.0):
            cur, order, fin = v, new, f2
            if v < best[0]:
                best = (v, new)
            if it % 16 == 0:
                order = sorted(order, key=lambda k: fin[0][k] - lates[0][k] - cost[0][k])
    return best[1]


ORDER = {}


def emit(g, T, ops):
    queue = {"v": g.vector, "a": g.scalar, "p": g.tensor, "s": g.sync, "g": g}
    deps = needs(ops)
    key = str([op[2:] for op in ops])
    if key not in ORDER:
        ORDER[key] = polish(ops, deps, arrange(ops, deps))
    order = ORDER[key]
    place = {k: i for i, k in enumerate(order)}
    deps = [{place[j] for j in deps[k]} for k in order]
    ops = [ops[k] for k in order]
    known, at_issue, waits = {}, [], []
    for k, op in enumerate(ops):
        eng, kind = op[0], op[4]
        kn = known.get(eng, 0)
        mine = []
        if kind != "arrive":
            for j in sorted(deps[k], reverse=True):
                if not kn >> j & 1:
                    mine.append(j)
                    kn |= at_issue[j] | 1 << j
            known[eng] = kn
        at_issue.append(kn if kind != "arrive" else 0)
        waits.append(mine)
    waiters = {}
    for k, w in enumerate(waits):
        for j in w:
            waiters.setdefault(j, []).append(k)
    team = {}
    for j in sorted(waiters):
        if ops[j][4] == "c":
            team.setdefault(tuple(waiters[j]), []).append(j)
    signal, last, count, ndma, tail, sent = {}, [0] * NPOOL, [0] * NPOOL, 0, [], 0
    for k, op in enumerate(ops):
        eng, fn, kind = op[0], op[1], op[4]
        q = queue.get(eng)
        if kind == "arrive":
            signal[k] = fn
            continue
        seen = []
        for j in waits[k]:
            if not any(signal[j] is z for z in seen):
                seen.append(signal[j])
                q.wait_ge(signal[j][0], signal[j][1])
        ins = fn(q)
        if kind == "remote":
            sent += ins
        elif kind == "dma":
            sem = T.sem["d%d" % ndma]
            ndma += 1
            ins.then_inc(sem, 16)
            signal[k] = (sem, 16)
            if k not in waiters:
                tail.append(signal[k])
        elif k in waiters:
            if k not in signal:
                mates = team[tuple(waiters[k])]
                s = min((z for z in range(NPOOL) if all(last[z] & ~at_issue[j] == 0 for j in mates)), key=lambda z: last[z])
                last[s] = sum(1 << j for j in mates)
                count[s] += len(mates)
                both = (T.sem["c%d" % s], count[s])
                for j in mates:
                    signal[j] = both
            ins.then_inc(signal[k][0], 1)
    g.wait_ge(T.sem.sent, sent)
    for sem, n in tail:
        g.wait_ge(sem, n)


def rank_program(g, core, T, topo):
    rank = T.rank_of(core)
    if rank is None:
        return
    N = len(T.cores)
    A, ACT = AluOpType, ActivationFunctionType
    ops = []

    def ap(v):
        if v[0] == "@":
            w = ap(v[1])
            if SCRATCH[v[1][0]][2] == X4:
                w = w.bitcast(dt.uint32)
            return w.indirect(ap(v[2]))
        return T[v[0]][:, v[1]:v[2]] if v[3] == 1 else T[v[0]][:, v[1]:v[2]:v[3]]

    def parts(*vs):
        out = []
        for v in vs:
            if isinstance(v, tuple):
                out += [v[1], v[2]] if v[0] == "@" else [v]
        return out

    def arg(s):
        return ap(s) if isinstance(s, tuple) else s

    def by(win, off):
        return ("@", win, off)

    def size(v):
        return 16 * size(v[2]) if v[0] == "@" else len(range(v[1], v[2], v[3]))

    def ns(out, a, *more, rate=1.0):
        if out[0] == "@" or a[0] == "@":
            return 55.0 + size(a) * (3.2 if out[0] == "@" else 1.3)
        if all(SCRATCH[v[0]][2] in (B, U) for v in parts(out, a, *more)):
            rate /= 2
        return 0.83 * max(64.0, size(a) * rate)

    def put(eng, fn, rd, wr, t, kind="c", boost=0.0):
        ops.append((eng, fn, rd, wr, kind, t + Z["each"][eng == "a"], boost))

    def copy(out, src, eng="v"):
        if eng == "a":
            act(out, src)
        elif out[0] == "@":
            put("v", lambda q: q.tensor_copy(ap(out), ap(src)), parts(src, out[2]), [out[1]], ns(out, src))
        elif SCRATCH[out[0]][2] == X4:
            put("v", lambda q: q.tensor_copy(ap(out).bitcast(dt.uint32), ap(src)), parts(src), [out], ns(out, src))
        else:
            put("v", lambda q: q.tensor_copy(ap(out), ap(src)), parts(src), [out], ns(out, src))

    def ts(out, a, s1, o1, s2=None, o2=None):
        if o2 is None:
            put("v", lambda q: q.tensor_scalar(ap(out), ap(a), arg(s1), None, o1), parts(a, s1), [out], ns(out, a, s1))
        else:
            put("v", lambda q: q.tensor_scalar(ap(out), ap(a), arg(s1), arg(s2), o1, o2), parts(a, s1, s2), [out], ns(out, a, s1, s2))

    def tt(out, a, b, o):
        both = a[0] != "@" and SCRATCH[a[0]][0] == "sbuf"
        put("v", lambda q: q.tensor_tensor(ap(out), ap(a), ap(b), o), parts(a, b), [out], ns(out, a, b, rate=2.0 if both else 1.0))

    def scan(out, d0, d1, init, o0, o1):
        put("v", lambda q: q.tensor_tensor_scan(ap(out), ap(d0), ap(d1), arg(init), o0, o1), parts(d0, d1, init), [out], ns(out, d0, d1))

    def turn(out, a):
        put("v", lambda q: q.transpose(ap(out), ap(a)), [a], [out], ns(out, a))

    def fill(out, c):
        put("v", lambda q: q.memset(ap(out), c), [], [out], ns(out, out))

    def quant(q_, s_, a, boost=0.0):
        put("v", lambda q: q.quantize_mx(ap(q_), ap(s_), ap(a)), [a], [q_, s_], 12.0 + 0.22 * size(a), boost=boost)

    def act(out, a, func=ACT.Copy, scale=None, bias=None, acc=None):
        kw = {}
        if scale is not None:
            kw["scale"] = arg(scale)
        if bias is not None:
            kw["bias"] = arg(bias)
        if acc is not None:
            kw["accum_out"] = ap(acc)
        t = 65.0 + 1.3 * size(a) if a[0] == "@" else 0.83 * max(64, size(a)) + (20.0 if acc else 0.0)
        put("a", lambda q: q.activation(ap(out), ap(a), func, **kw), parts(a, scale, bias), parts(out, acc), t)

    def mm(out, wq, wsc, xq, xsc):
        put("p", lambda q: q.matmul_mx(ap(out), ap(wq), ap(wsc), ap(xq), ap(xsc), True, True), [wq, wsc, xq, xsc], [out], 60.0)

    def iota(out, pattern, base=0, cm=0):
        t = 130.0 + 1.66 * size(out)
        if SCRATCH[out[0]][2] == I:
            put("g", lambda q: q.iota(ap(out), pattern, base, cm), [], [out], t)
        else:
            put("g", lambda q: q.iota(ap(out), pattern, base, cm, allow_small_or_imprecise_dtypes=True), [], [out], t)

    def zero(out):
        iota(out, [[0, size(out)]])

    def heads(out, src, n, w, c):
        put("g", lambda q: q.affine_select(ap(out), ap(src), [[0, n], [1, w]], A.is_gt, c, 0, 0), [src], [out], 170.0 + 1.66 * n * w)

    def dma(eng, out, src, rd, wr, t=50.0):
        put(eng, lambda q: q.dma_start(out, src), rd, wr, t, "dma")

    def col(k):
        return V("col", k, k + 1)

    def ends(name, n, w, lo=0):
        return V(name, lo * w + w - 1, n * w, w)

    def gather(out, win, lst, share, lo, hi, shift=0):
        cut = lo + 2 * int((hi - lo) * share / 2 + 0.5)
        for eng, a, b in (("v", lo, cut), ("a", cut, hi)):
            if b > a:
                copy(V(out, shift + 16 * a, shift + 16 * b), by(win, V(lst, a, b)), eng)

    cH, cE, cA, cJ, cA4, cT, cS4, cS16, cS1, c2A, cTH, cU, cU4, cN, cN2, cX, cY, cA1, cN3, cT8 = range(20)
    WHOLE, PARTS = ((0, H),), ((0, 64), (64, H))

    dma("s", ap(V("X0", 0, 384)), T.x[:, 0:384], [], [V("X0", 0, 384)])
    dma("a", ap(V("X", 384, 768)), T.x[:, 384:768], [], [V("X", 384, 768)], 250.0)
    dma("s", ap(V("X", 0, 384)), T.x[:, 0:384], [], [V("X", 0, 384)])
    dma("s", ap(V("qw")).bitcast(dt.uint8), T.wc[:, :], [], [V("qw")])
    dma("s", ap(V("sw")), T.ws[:, :], [], [V("sw")])
    dma("s", ap(V("vt")), T.v[:, :], [], [V("vt")])

    iota(V("ip", 0, 1), [[0, 1]], 0, 1)
    iota(V("ip", 1, 2), [[0, 1]], 127, -1)
    iota(V("iu"), [[0, 3], [4096, 4], [0, 2]], 128 * 127 + 4096, -127)
    iota(V("rl"), [[32, 3], [0, 4], [16, 2]])
    iota(V("k16"), [[0, 6], [1, 16]])
    iota(V("irep", 0, 6), [[32, 6]], 31)
    iota(V("irep", 6, 12), [[4, 6]], 3)
    iota(V("irep", 12, 16), [[32, 2], [64, 2]], 31)
    iota(V("irep", 16, 18), [[32, 2]], 31)
    iota(V("k4"), [[0, 48], [1, 4]])
    iota(V("k32"), [[0, 2], [1, 32]])
    iota(V("k2"), [[1, 32], [0, 2]])
    fill(V("one"), 1.0)
    fill(V("big"), HUGE)
    heads(V("t32"), V("big"), 6, 32, TINY)
    heads(V("r32"), V("one"), 3, 32, 0.0)
    heads(V("r16"), V("one"), 6, 16, 0.0)
    iota(V("vals"), [[1, C]])
    iota(V("ka4"), [[0, 6], [1, 4], [0, 4]])
    iota(V("base"), [[8, 24], [0, 4]])
    iota(V("r4"), [[0, 8], [64, 4]])
    for v in (V("th", 24, 32), V("cz", 0, C, 2), V("zt"), V("SX", 768, 776), V("AR", 512, 528),
              V("AR", 784, 1040), V("Mt", 384, 512)):
        zero(v)

    def same(out, a, c):
        act(out, a, ACT.Abs, scale=-1.0, bias=c)
        act(out, out, ACT.Relu, scale=-1.0, bias=1.0)

    def radix(out, k, tmp, c):
        act(tmp, k, ACT.Sign, bias=c)
        act(tmp, tmp, ACT.Abs, scale=RADIX + 1.0, bias=col(cX))
        act(out, tmp, ACT.Abs, bias=col(cY))

    fill(V("X", 768, 896), 0.0)
    fill(col(cX), 0.5)
    fill(col(cY), -RADIX - 0.5)
    ts(V("ic", 0, 2), V("ip"), 4, A.logical_shift_right, 1, A.bitwise_and)
    copy(V("colb"), V("ic", 0, 2))
    copy(V("col", 0, 2), V("ic", 0, 2))
    for k, (sh, m) in enumerate([(0, 15), (0, 31), (2, 3), (0, 3)]):
        ts(V("ic", 2 + k, 3 + k), V("ip", 0, 1), sh, A.logical_shift_right, m, A.bitwise_and)
    copy(V("col", 2, 6), V("ic", 2, 6))
    ts(V("iw"), V("iu"), 3 * 4096 + 15, A.bitwise_and)
    tt(V("rq"), V("iw"), V("rl"), A.add)
    fill(V("X0", 384, 512), 0.0)
    ts(V("op1"), V("rq"), float(H), A.min)
    ts(V("opf", 0, 16), V("rq", 0, 16), 64.0, A.min, 2.0, A.mult)
    ts(V("opf", 16, 24), V("rq", 0, 8), 32.0, A.min, 2.0, A.mult)
    ts(V("op3"), V("rq"), float(H), A.min, 2.0, A.mult)
    ts(V("op4"), V("opf"), 1.0, A.add)
    ts(col(cN2), col(cA4), 2.0, A.is_ge, -96.0, A.mult)
    act(col(cN), col(cA4), ACT.Identity, scale=64.0, bias=col(cN2))
    ts(V("on4", 0, 1), col(cN), 31.0, A.add)
    act(col(cN3), col(cA4), ACT.Identity, scale=32.0, bias=31.0)
    ts(V("on4", 2, 3), col(cN3), 63.0, A.min)
    ts(col(cS1), col(cA4), 3.0, A.is_equal, 1.0 / RADIX, A.max)
    ts(col(cS16), col(cA), 15.0, A.is_equal, 1.0 / RADIX, A.max)
    act(col(cU), col(cA), ACT.Identity, scale=-1.0, bias=-1.0)
    act(col(cU4), col(cA4), ACT.Identity, scale=-1.0, bias=-1.0)
    act(col(cA1), col(cA), ACT.Identity, bias=-0.5)
    ts(V("d16"), V("k16"), col(cA), A.is_equal)
    ts(V("eye"), V("k32"), col(cJ), A.is_equal)
    same(V("eye2"), V("k2"), col(cJ))
    radix(V("g16"), V("k16"), V("s16"), col(cU))
    radix(V("g4"), V("k4"), V("k4"), col(cU4))
    copy(V("orep", 0, 18), V("irep", 0, 18))
    act(V("mul"), V("k16"), ACT.Sign, scale=-1.0, bias=col(cA1))
    act(V("mul"), V("mul"), ACT.Relu, scale=1.0 - BELOW)
    act(V("mul"), V("mul"), ACT.Identity, scale=-1.0, bias=1.0)
    act(col(cS4), col(cS1), scale=4.0)
    act(col(c2A), col(cA4), scale=2.0)
    act(col(cTH), col(cT), scale=HUGE)
    act(V("ka4"), V("ka4"), ACT.Abs, scale=-HUGE, bias=col(cTH))
    act(V("base"), V("base"), ACT.Identity, bias=col(c2A))
    act(V("b2"), ends("base", 24, 4), ACT.Identity, scale=2.0, bias=1.0)

    PK, PG = ["pk0", "pk1", "pk2"], ["pg0", "pg1", "pg2"]

    def mask(out, src, h, eng):
        if eng == "a":
            act(out, src, scale=col(cE if h == 0 else cH))
        else:
            ts(out, src, V("colb", 1 - h, 2 - h), A.mult)

    def products(k, kind, a, e, qf, sf, lst, banks, eye):
        n = max(128, 2 * (e - a))
        lo, at = 2 * e - n, 2 * a
        quant(V("qg" + kind, at, at + n), V("sg" + kind, at, at + n), V("G" + kind, 4 * lo, 4 * (lo + n)), Z["boost"])
        for x, y in PARTS:
            if a <= x and y <= e:
                copy(V("qs%d" % k, 4 * x, 4 * y), by(qf, V(lst, x // 4, y // 4)))
                act(V("ss%d" % k, 4 * x, 4 * y), by(sf, V(lst, x // 4, y // 4)))
        for b in range(a // 32, e // 32):
            c = 64 * b - lo
            w = min(c, n - 128)
            mm(V(banks[b], 0, 128), V("qs%d" % k, 128 * b, 128 * b + 128), V("ss%d" % k, 128 * b, 128 * b + 128),
               V("qg" + kind, at + w, at + w + 128), V("sg" + kind, at + w, at + w + 128))
            tt(V("D" + kind, 64 * b, 64 * b + 64), V(banks[b], c - w, c - w + 64), V(eye), A.mult)

    def sizes(k, kind, a, e, name, lo, qf, sf, lst, banks, share):
        todo = [(b, h) for b in range(a // 32, e // 32) for h in range(2)]
        for n, (b, h) in enumerate(todo):
            mask(V("G" + kind, 256 * b + 128 * h, 256 * b + 128 * h + 128), V(name, lo + 128 * b, lo + 128 * b + 128), h,
                 "a" if n < share * len(todo) else "v")
        products(k, kind, a, e, qf, sf, lst, banks, "eye")
        for x, y in PARTS:
            if a <= x and y <= e:
                w = 64 if k > 1 else 2 * (y - x)
                for c in range(2 * x, 2 * y, w):
                    scan(V("E" + kind, c, c + w), V("t32", c, c + w), V("D" + kind, c, c + w), 1.0, A.min, A.add)
                src = by(V("E" + kind, 2 * x, 2 * y), V("orep", 0, (y - x) // 16))
                tt(V("prw" + kind, x, y), src, V("d16", x, y), A.mult)
                copy(V("pre" + kind, x, y), src, "a")

    def place(a):
        return 8 * a + (16 if a >= 64 else 0)

    def paired(k, kind, name, lst, banks, nact):
        gap = 4 if kind == "R" else 0
        if gap:
            wins = [(V("qf%d" % k, 0, 130), V("sf%d" % k, 0, 130)), (V("qf%d" % k, 160, 288), V("sf%d" % k, 160, 288))]
            quant(*wins[0], V(name, 0, 520))
            quant(*wins[1], V(name, 528, 1040))
        else:
            wins = [(V("qf%d" % k, 0, C + 2), V("sf%d" % k, 0, C + 2))] * 2
            quant(*wins[0], V(name))
        hi = 4 * (C + gap)
        for n, (u, h) in enumerate([(u, h) for u in range(4) for h in range(2)]):
            mask(V("G" + kind, 4 * h + u, hi, 8), V(name, 4 + u, hi, 8), h, "a" if n < nact else "v")
        quant(V("qg" + kind, 0, C + gap), V("sg" + kind, 0, C + gap), V("G" + kind, 0, hi), Z["boost"])
        for (x, y), (qf, sf) in zip(PARTS, wins):
            copy(V("qs%d" % k, 4 * x, 4 * y), by(qf, V(lst, x // 4, y // 4)))
            act(V("ss%d" % k, 4 * x, 4 * y), by(sf, V(lst, x // 4, y // 4)))
        for b, w, c in ((0, 0, 0), (1, 0, 64), (2, 64 + gap, 64)):
            mm(V(banks[b], 0, 128), V("qs%d" % k, 128 * b, 128 * b + 128), V("ss%d" % k, 128 * b, 128 * b + 128),
               V("qg" + kind, w, w + 128), V("sg" + kind, w, w + 128))
            tt(V("D" + kind, 64 * b, 64 * b + 64), V(banks[b], c, c + 64), V("eye2"), A.mult)
        for a, e in PARTS:
            for h in range(2):
                lo = 2 * a + h * (e - a)
                out, d = V("E" + kind, lo, lo + e - a), V("D" + kind, 2 * a + h, 2 * e, 2)
                if kind == "A":
                    scan(out, V("r32", a, e), d, 0.0, A.mult, A.add)
                else:
                    scan(out, V("t32", a, e), d, 1.0, A.min, A.add)

    def spread(kind, row, lo):
        for a, e in (PARTS if Z["pk"] > 1 and kind == "K" else WHOLE):
            turn(V("own" + kind, a, e), V("prw" + kind, a, e))
            turn(V(row, lo + a, lo + e), V("pre" + kind, a, e))
            scan(V("ow" + kind, a, e), V("r16", a, e), V("own" + kind, a, e), 0.0, A.mult, A.add)
            tt(V("mix" + kind, a, e), V(row, lo + a, lo + e), V("mul", a, e), A.mult)

    def count(on_act, ws, o, signs, flags, res, more=None):
        name, at = res
        buf, lo = signs if on_act else flags
        n = 0
        for w in ws:
            out = V(buf, lo + n, lo + n + size(w))
            n += size(w)
            if on_act:
                act(out, w, ACT.Sign, scale=-1.0, bias=o)
            else:
                ts(out, w, o, A.is_lt)
        if on_act:
            s = V(buf, lo, lo + n + (1 if more else 0))
            act(s, s, ACT.Relu, acc=V(name, at, at + 1))
        else:
            scan(V(name, at + 1 - n // 2, at + 1), V(buf, lo, lo + n // 2), V(buf, lo + n // 2, lo + n), more or 0.0, A.add, A.add)

    def end16(name, m):
        return V(name, 16 * m + 15, 16 * m + 16)

    def old_half(row):
        spread("S", row, 0)
        act(V("row", C, C + H), V(row, 0, H), scale=BELOW)
        if row == "rs":
            act(V("rs", H, H + WS), V("rs", 0, WS), scale=BELOW)
            act(V("row", 0, H), V("rs", 0, H))
            for m in range(CH):
                count(m < Z["ss"], [V("rs", 16 + 16 * m, 16 + 16 * m + WS), V("mixS", 16 * m, 16 * m + 16)], end16("owS", m),
                      ("snS", H * m), ("fs", H * m), ("sn", (H + 1) * m + H))

    def new_half(t):
        spread("K", "row", H)
        act(V("row", C + H, C + H + WS), V("row", H, H + WS), scale=BELOW)
        nkk = Z["kk" if t else "kk0"]
        first = len(ops)
        for m in range(CH):
            at, res = (H + 1) * m, ("fin", SLOT * m + SLOT - 1)
            if t == 0:
                count(m < Z["sk0"], [V("row", 16 + 16 * m, 16 + 16 * m + WK), V("mixS", 16 * m, 16 * m + 16)], end16("owS", m),
                      ("snW", C * m), ("fw", C * m), res)
            else:
                count(m < Z["sk"], [V("row", H, C)], end16("owS", m), ("sn", at), ("fx", H * m), res, V("sn", at + H, at + H + 1))
        copy(V("ork", 0, CH), ends("fin", CH, SLOT))
        ops[first:] = [op[:6] + (Z["early"],) for op in ops[first:]]
        copy(by(V("O"), V("ork", 0, CH)), V("vals", 0, H))
        ops[-1] = ops[-1][:6] + (Z["late"],)
        for m in range(CH):
            res = ("fin", SLOT * (CH + m) + SLOT - 1) if m < nkk else ("cn", SLOT * m + SLOT - 1)
            lo = H + 16 + 16 * m
            count(m < nkk, [V("row", lo, lo + WK), V("mixK", 16 * m, 16 * m + 16)], end16("owK", m), ("snK", C * m), ("fk", C * m), res)
        copy(V("ork", CH, CH + nkk), ends("fin", CH + nkk, SLOT, CH))
        copy(V("ork", CH + nkk, 12), ends("cn", CH, SLOT, nkk))
        copy(by(V("O"), V("ork", CH, 12)), V("vals", H, C))

    quant(V("qf0", 0, 128), V("sf0", 0, 128), V("X0"))
    sizes(0, "S", 0, H, "X0", 0, V("qf0", 0, 128), V("sf0", 0, 128), "op1", PK, Z["mk0"][0])
    quant(V("qf0", 128, 256), V("sf0", 128, 256), V("X", 384, 896))
    sizes(1, "K", 0, H, "X", 384, V("qf0", 128, 256), V("sf0", 128, 256), "op1", PG, Z["mk0"][1])
    old_half("row")

    for t in range(R):
        stage = 2 + 3 * t
        new_half(t)
        scan(V("lx"), V("g4"), V("O"), 0.0, A.mult, A.add)
        scan(V("ld"), V("g16"), V("O", 0, C, 2), 0.0, A.mult, A.add)
        ts(V("ox"), ends("lx", 48, 4), col(cS4), A.mult, col(cT), A.add)
        ts(V("od"), ends("ld", CH, 16), col(cS16), A.mult)
        gather("SX", V("X", 0, 768), "ox", 0.5, 0, 48)
        if t == R - 1:
            act(V("Of"), V("O"))
            dma("s", T.ol[:, :], T.Of[0:128:16, :], [V("Of")], [])
        act(V("da"), by(V("row", 0, C), V("od")))
        turn(V("dap"), V("da"))
        d6 = V("dap", 0, H, 16)
        act(V("th", 0, 24, 4), d6, scale=0.75)
        act(V("th", 1, 24, 4), d6, scale=0.25)
        act(V("th", 3, 24, 4), V("th", 0, 24, 4), scale=-BELOW)
        act(V("th", 2, 24, 4), V("th", 1, 24, 4), scale=-BELOW)
        tt(V("dam"), V("dap"), V("ka4"), A.max)
        dst = T.cores[(rank + STEP[t]) % N]
        src = T.cores[(rank - STEP[t]) % N]
        rid, pid = topo.addr(dst, core)
        at = 128 + H * t
        qm, sm = "qm%d" % t, "sm%d" % t

        def share(a, b, k, t=t):
            return topo.engines(a, b)[k::2] if t == 0 else topo.engines(a, b)

        def send(out, src, arr, engines, rid=rid, pid=pid):
            def go(q):
                q.remote_dma(out, src, arr, T.sem.sent, pid, rid, sum(1 << e for e in engines))
                return len(engines)
            return go

        paired(stage, "A", "SX", "op3", PK, Z["ma"])

        for s, (a, e) in enumerate(PARTS):
            cp, cq = V("cp", 16 * s, 16 * s + 16), V("cq", 16 * s, 16 * s + 16)
            tt(cp, by(V("EA", 2 * a, 2 * e), V("on4", 2 * s, 2 * s + 1)), V("th", 16 * s, 16 * s + 16), A.is_ge)
            scan(cq, V("r4", 0, 16), cp, 0.0, A.min, A.add)
            ts(V("ncp", a, e), by(cq, V("orep", 6, 6 + (e - a) // 16)), -0.5, A.mult, 1.0, A.add)
            turn(V("cz", 2 * a + 1, 2 * e, 2), V("ncp", a, e))
            lo = place(a)
            hi = lo + 8 * (e - a)
            for u in range(4):
                scan(V("AR", lo + u, hi, 4), V("cz", 2 * a, 2 * e), V("SX", 8 * a + u, 8 * e, 4), 0.0, A.mult, A.add)

        paired(stage + 1, "R", "AR", "op4", PG, Z["mr"])
        for s, (a, e) in enumerate(PARTS):
            lo = place(a)
            hi = lo + 8 * (e - a)
            rep = V("orep", 12 + a // 16, 12 + e // 16)
            tt(V("swp", a, e), by(V("ER", 2 * a, 2 * e), rep), V("dam", a, e), A.is_ge)
            turn(V("swr", a, e), V("swp", a, e))
            scan(V("lm", a, e), V("base", 0, e - a), V("swr", a, e), 0.0, A.max, A.add)
            ts(V("om", a // 4, e // 4), ends("lm", e // 4, 4, a // 4), 4.0, A.mult, col(cT), A.add)
            gather("Mt", V("AR", lo, hi), "om", Z["gm"][s], a // 4, e // 4)
            if Z["sends"][t] == 2 or s:
                x = a if Z["sends"][t] == 2 else 0
                quant(V(qm, 2 * x, 2 * x + 128), V(sm, 2 * x, 2 * x + 128), V("Mt", 4 * x, 4 * x + 512))
                arr = T.sem["arr%d" % (2 * t + s)]
                lq, ls = V("ql", at + x, at + e), V("sl", at + x, at + e)
                mq, ms = V(qm, 2 * x, x + e), V(sm, 2 * x, x + e)
                put("g", send(ap(lq).bitcast(dt.uint8), ap(mq).bitcast(dt.uint8), arr, share(core, dst, 0)), [mq], [], 100.0, "remote")
                put("g", send(ap(ls), ap(ms), arr, share(core, dst, 1)), [ms], [], 100.0, "remote")
                put("x", (arr, len(share(src, core, 0) + share(src, core, 1))), [mq], [lq, ls], Z["send"], "arrive")

            tt(V("ls", a // 4, e // 4), V("b2", 0, (e - a) // 4), ends("lm", e // 4, 4, a // 4), A.subtract)
            ts(V("oz", a // 4, e // 4), V("ls", a // 4, e // 4), 4.0, A.mult, col(cT), A.add)
            gather("X", V("AR", lo, hi), "oz", 0.0, a // 4, e // 4)
            if t < R - 1:
                tt(V("preS", a, e), by(V("ER", 2 * a, 2 * e), rep), V("dap", a, e), A.min)

        if t == 0:
            quant(V("ql", 0, 128), V("sl", 0, 128), V("zt"))
        if t < R - 1:
            tt(V("prwS"), V("preS"), V("d16"), A.mult)
            old_half("rs")
        else:
            quant(V("qv"), V("sv"), V("vt"))
            quant(V("qxs"), V("sxs"), V("X", 0, 512))
            mm(V("py", 0, 128), V("qv"), V("sv"), V("qxs"), V("sxs"))
            dma("s", T.oc[:, 0:4 * H], ap(V("qxs", 0, H)).bitcast(dt.uint8), [V("qxs")], [])
            for e in range(4):
                dma("s", T.osc[4 * e:4 * e + 4, 0:H], T.sxs[32 * e:32 * e + 4, 0:H], [V("sxs")], [])
            copy(V("yt", 0, H), V("py", 0, H))
            dma("s", T.y[:, 0:H], ap(V("yt", 0, H)), [V("yt", 0, H)], [])

        for a, e in (PARTS if Z["sends"][t] == 2 else WHOLE):
            for b in (2, 0, 3, 1):
                mm(V("pk%d" % b, 0, 128), V("qw", 128 * b, 128 * b + 128), V("sw", 128 * b, 128 * b + 128),
                   V("ql", at + e - 128, at + e), V("sl", at + e - 128, at + e))
            for b in (0, 1):
                ts(V("X", 384 + 4 * a + b, 384 + 4 * e, 4), V("pk%d" % b, 128 - e + a, 128), 0.03125, A.mult)
                act(V("X", 386 + 4 * a + b, 384 + 4 * e, 4), V("pk%d" % (b + 2), 128 - e + a, 128), scale=0.03125)
            if t < R - 1:
                qf, sf = V("qf%d" % (stage + 2), 2 * a, 2 * a + 128), V("sf%d" % (stage + 2), 2 * a, 2 * a + 128)
                quant(qf, sf, V("X", 384, 896))
                sizes(stage + 2, "K", a, e, "X", 384, qf, sf, "op1", PG, Z["mk"])

    quant(V("qxk"), V("sxk"), V("X", 384, 896))
    mm(V("pg0", 0, 128), V("qv"), V("sv"), V("qxk"), V("sxk"))
    dma("s", T.oc[:, 4 * H:4 * C], ap(V("qxk", 0, H)).bitcast(dt.uint8), [V("qxk")], [])
    for e in range(4):
        dma("s" if e < 2 else "a", T.osc[4 * e:4 * e + 4, H:C], T.sxk[32 * e:32 * e + 4, 0:H], [V("sxk")], [])
    copy(V("yt", H, C), V("pg0", 0, H))
    dma("a", T.y[:, H:C], ap(V("yt", H, C)), [V("yt", H, C)], [])
    emit(g, T, ops)
